import numpy as np, ml_dtypes
CORES = [6,15,38,47]
N = 4
import mx_ref
BF = ml_dtypes.bfloat16
def gentries(a):
    return np.ascontiguousarray(a.reshape(8, 16, -1).transpose(0, 2, 1)).reshape(8, -1)
def gtable(e):
    e = np.asarray(e); return np.ascontiguousarray(e.reshape(8, -1, 16).transpose(0, 2, 1)).reshape(128, -1).astype(np.int32)
def gcols(t, e):
    v = np.concatenate([t.reshape(8, 16, -1, 4), np.zeros((8, 16, 1, 4), BF)], axis=2)
    return np.ascontiguousarray(np.stack([v[g][:, e[g]] for g in range(8)])).reshape(128, -1)
def tile(rs):
    return np.stack(rs, axis=2).reshape(128, -1).astype(BF)
def pick(q, e):
    c = np.concatenate([q[0].reshape(128, -1, 4), np.zeros((128, 1, 4), np.uint8)], axis=1); s = np.concatenate([q[1], np.ones((16, 1), np.uint8)], axis=1)
    return (np.ascontiguousarray(c[:, e].reshape(128, -1)), np.ascontiguousarray(s[:, e]))
def join(*qs):
    return (np.concatenate([q[0] for q in qs], axis=1), np.concatenate([q[1] for q in qs], axis=1))
def put(q, e, v):
    c, s = q[0].reshape(128, -1, 4).copy(), q[1].copy(); c[:, e] = v[0].reshape(128, -1, 4); s[:, e] = v[1]
    return (c.reshape(128, -1), s)
def pk(c, s):
    return (np.ascontiguousarray(c), mx_ref.live(s))
def emit(q):
    return q[0], q[1]
def packed(v, rng):
    q = [mx_ref.quantize(np.ascontiguousarray(v[r])) for r in range(N)]
    return np.stack([a for a, b in q]), np.stack([mx_ref.plane(b, rng) for a, b in q])
def values_of_codes():
    e, c = np.zeros((128, 128, 4), np.float32), np.zeros((128, 2, 4), np.uint8)
    e[np.arange(128), np.arange(128), 0] = 1
    c[:127, :, 0] = np.arange(256).reshape(2, 128).T[:127]
    return mx_ref.matmul(mx_ref.quantize(e.reshape(128, 512).astype(BF)), (c.reshape(128, 8), np.full((16, 2), 127, np.uint8))).T.reshape(-1).astype(np.float64)
CODE_VALUE, SCALE_VALUE = values_of_codes(), 2.0 ** (np.arange(256) - 127.0)
def decode(q):
    return (CODE_VALUE[q[0]].reshape(16, 8, -1, 4) * SCALE_VALUE[q[1]][:, None, :, None] + 0.0).reshape(128, -1).astype(np.float32)
def f(rng, *shape):
    return mx_ref.flush((rng.standard_normal(shape, dtype=np.float32) * np.exp2(rng.integers(-2, 3, shape[:-1] + (1,)))).astype(BF))
def wide(rng, *shape, cols=0):
    v = rng.standard_normal(shape, dtype=np.float32) * np.exp2(rng.integers(-12, 13, shape)).astype(np.float32)
    if cols: v *= np.repeat(np.exp2(rng.integers(-cols, cols + 1, shape[:-2] + (1, shape[-1] // 4))) * (rng.random(shape[:-2] + (1, shape[-1] // 4)) > 0.0625), 4, axis=-1).astype(np.float32)
    return mx_ref.flush(v.astype(BF))
C = 448
STEP = [1, 2, 3]
def take(a, e):
    return np.take_along_axis(a, e, axis=-1)
def effective(back):
    e = np.ones(back.shape, bool)
    for j in range(C - 1, -1, -1):
        up = back[..., j]
        e[..., j] = (up <= j) | ~take(e, up[..., None])[..., 0]
    return e
def numbers_of(rng):
    return {"x": np.array(f(rng, N, 128, 4 * C)), "u": np.array(f(rng, N, 128, 512)), "v": np.array(f(rng, N, 128, 512))}
def stored(back, ring, mate):
    return {k: np.stack([gtable(e[r]) for r in range(N)]) for k, e in (("ud", np.argsort(back, axis=-1)), ("iv", back), ("hp", ring), ("mt", mate))}
def shuffled(rng):
    return rng.permuted(np.tile(np.arange(C), (N, 8, 1)), axis=2)
def linked(order):
    e = np.zeros_like(order)
    np.put_along_axis(e, order, np.roll(order, -1, axis=-1), axis=-1)
    return e
def mates(rng):
    a = shuffled(rng)
    e = np.zeros_like(a)
    np.put_along_axis(e, a[..., ::2], a[..., 1::2], axis=-1)
    np.put_along_axis(e, a[..., 1::2], a[..., ::2], axis=-1)
    return e
def runs(rng, back):
    return linked(np.argsort(effective(back) + rng.random(back.shape), axis=-1))
def lists(rng):
    return stored(shuffled(rng), linked(shuffled(rng)), mates(rng))
def layers(rng, still=()):
    w = np.array(f(rng, N, 128, 2048)).reshape(N, 8, 16, 4, 8, 16, 4)
    for i in still:
        w[:, :, i] = 0
        w[:, :, :, :, :, i] = 0
    return w
def weights(rng, w):
    c, s = packed(np.ascontiguousarray(w).reshape(N, 128, 2048), rng)
    return {"wc": c, "ws": s}
def setup_inputs(rng):
    return {**numbers_of(rng), **lists(rng), **weights(rng, layers(rng))}
def setup_inputs_ties(rng):
    d = numbers_of(rng)
    o = rng.permutation(N)
    k = rng.choice([-1.0, 0.0, 1.0, 1.0], (N, 8, C))
    k[o[0]] = 0
    k[o[1]] = 1
    k[o[2]] = (rng.permutation(8) % 2 * 2.0 - 1.0)[:, None]
    x = d["x"].reshape(N, 8, 16, C, 4)
    x[:, :, 0] = 0
    x[:, :, 0, :, 0] = k.astype(np.float32).astype(BF)
    u = d["u"].reshape(N, 128, 128, 4)
    u[:, :, ::16] = 0
    for h in range(0, 128, 16): u[:, h, h, 0] = 1
    back = np.zeros((N, 8, C), np.int64)
    for r in range(N):
        for g, m in enumerate(rng.permutation([1, 1, 1, 2, 2, 3, C // 8, 0])):
            a = rng.integers(0, m, C) if m else np.arange(C)
            for i in np.unique(a):
                e = np.flatnonzero(a == i)
                back[r, g, e] = np.roll(e, -1)
    mate = mates(rng)
    tau = np.where((k > 0) & (take(k, mate) > 0), mate, np.arange(C))
    return {"x": x.reshape(N, 128, 4 * C), "u": u.reshape(N, 128, 512), "v": d["v"], **stored(take(tau, back), runs(rng, back), mate), **weights(rng, layers(rng, [0]))}
def setup_inputs_near(rng):
    d = numbers_of(rng)
    i = np.arange(N)
    first = np.minimum(i, i ^ STEP[0])
    small = np.isin(first, rng.permutation(np.unique(first))[:N // 4])
    k = np.where(small, 2.0 ** -30, 1.0)
    x = d["x"].astype(np.float32).reshape(N, 8, 16, C, 4)
    x[:, :, :8] = 0
    s = rng.choice([-1.0, 0.0, 1.0, 1.0], (N, 8, C)) * k[:, None, None]
    x[:, :, 0, :, 0] = 1.125 * s
    x[:, :, 1, :, 0] = -1.25 * s
    x[:, :, 3, :, 0] = np.where(small[:, None, None], rng.choice([-1.0, 1.0], (N, 8, C)) * 2.0 ** -30, 0.0)
    x[:, :, 4, :, 0] = np.where(small, 2.0 ** -27, 0.0)[:, None, None]
    u = d["u"].reshape(N, 128, 128, 4)
    u[:, :, ::16] = 0
    w = layers(rng, range(8))
    for r in range(N):
        at = [0, C - 1, int(rng.integers(C)), int(rng.integers(C))]
        for g, j in zip(rng.permutation(8)[:4], at): x[r, g, 0, j, 0] = 2.0 ** 30 * rng.choice([-1.0, 1.0])
        for g in range(8):
            h = 16 * g
            u[r, h, h, 0] = 1.125 * k[r]
            u[r, h + 1, h, 0] = k[r]
            u[r, h + 2, h, 0] = 1.125 * k[r]
            u[r, h + 5, h, 0] = k[r]
            if small[r]:
                w[r, g, 3, 0, g, 2, 0] = 2.0 ** -7
                w[r, g, 3, 0, g, 5, 0] = -2.0 ** -7
    return {"x": x.reshape(N, 128, 4 * C).astype(BF), "u": u.reshape(N, 128, 512), "v": d["v"], **lists(rng), **weights(rng, w)}
def setup_inputs_odd(rng):
    d = numbers_of(rng)
    x = (1.0 + (2 * rng.integers(0, 64, (N, 16, 8, C, 4)) + 1) * 2.0 ** -7) * np.exp2(-rng.integers(0, 7, (N, 16, 8, C, 4)).astype(np.float64)) * rng.choice([-1.0, 1.0], (N, 16, 8, C, 4))
    x[:, ::2] = 0
    x[:, :, 0, :, 0] = 1.96875 * 2.0 ** 8 * rng.choice([-1.0, 1.0], (N, 16, C))
    x[:, ::2, 1, :, 0] = (1.0 + 0.125 * (rng.random((N, 8, C)) < 0.75)) * 2.0 ** -5
    x[:, ::2, 2, :, 0] = (1.0 + 0.125 * (rng.random((N, 8, C)) < 0.25)) * 2.0 ** -5
    x[:, 14, 0, :, 1] = 16.0
    u = d["u"].reshape(N, 128, 128, 4)
    u[:, :, ::16] = 0
    for h in range(0, 128, 16):
        u[:, h + 1, h, 0] = 1
        u[:, h + 2, h, 0] = -1
        u[:, h + 3, h, 0] = 1
    w = layers(rng, [0, 1, 2, 8])
    w[:, 7, 0, 0, :, 0, 1] = -16.0
    return {"x": x.astype(np.float32).reshape(N, 128, 4 * C).astype(BF), "u": u.reshape(N, 128, 512), "v": d["v"], **lists(rng), **weights(rng, w)}
def setup_inputs_ends(rng):
    d = numbers_of(rng)
    x = np.zeros((N, 8, 16, C, 4))
    u = d["u"].astype(np.float32).reshape(N, 128, 128, 4)
    v = d["v"].astype(np.float32)
    w = np.zeros((N, 128, 4, 128, 4), np.float32)
    o, kinds = np.zeros(N, np.int64), rng.permutation(4)
    left = rng.permutation(np.unique(np.minimum(np.arange(N), np.arange(N) ^ STEP[0])))
    o[left] = kinds[:N // 2]
    o[left ^ STEP[0]] = kinds[(np.arange(N // 2) + 2) % 4]
    i, j = np.arange(128), np.arange(C)
    turns = np.stack([j ^ 1, C - 1 - j, (j + C // 2) % C])
    ways = np.stack([np.roll(j, -1), j, C - 1 - j, np.roll(j, 1)])
    mate = np.stack([turns[rng.permutation(8) % 3] for r in range(N)])
    plan = np.stack([ways[rng.permutation(8) % 4] for r in range(N)])
    ring, back = runs(rng, plan), plan.copy()
    for r in range(N):
        h = rng.permutation(8)
        sign = np.where(h < 2, 0.0, h % 2 * 2.0 - 1.0)
        c = sign[None, :, None]
        e = rng.permutation(8)
        ring[r, e[:2]] = np.roll(j, -1)
        ring[r, e[2:4]] = np.roll(j, 1)
        if o[r] in (0, 2): back[r, sign < 0] = take(mate[r], plan[r])[sign < 0]
        low = -(0.9 + 0.1 * rng.random((8, 16, C, 4))) * 2.0 ** 30
        if o[r] == 0: x[r] = low
        if o[r] == 1: x[r] = np.where((rng.random(C) < 0.5)[:, None], (1.0 + 0.4 * rng.random((8, 16, C, 4))) * 2.0 ** 27, low)
        if o[r] == 2: x[r] = -(1.0 + 0.125 * rng.integers(0, 8, (8, 16, C, 4))) * 2.0 ** -30
        if o[r] == 3: x[r] = d["x"][r].astype(np.float32).reshape(8, 16, C, 4)[:, :, :1]
        if o[r] < 2:
            x[r, 7, 15, :, 3] *= 2.0 ** -6
            u[r, :, ::16] = c * (0.9 + 0.1 * rng.random((128, 8, 4))) * 2.0 ** 30
            v[r] = rng.choice([-1.0, 1.0], (128, 512)) * (0.9 + 0.1 * rng.random((128, 512))) * 2.0 ** 30
        if o[r] == 2:
            u[r, :, ::16] = c * (1.0 + 0.125 * rng.integers(0, 8, (128, 8, 4))) * 2.0 ** -30
            v[r] = rng.choice([-1.0, 1.0], (128, 512)) * (1.0 + 0.125 * rng.integers(0, 8, (128, 512))) * 2.0 ** -30
        if o[r] == 3: u[r, :, ::16] *= np.abs(c).astype(np.float32)
        k = np.array([8.0, 16.0, 32.0])[rng.permutation(8) % 3]
        for b in range(4): w[r, i, b, i, b] = k[i // 16]
        if o[r] == 2:
            w[r, 127, 3, 127, 3] = 256.0
            w[r, 126, 3, 126, 3] = 2.0 ** -8
    return {"x": x.astype(np.float32).reshape(N, 128, 4 * C).astype(BF), "u": u.reshape(N, 128, 512).astype(BF), "v": v.astype(BF), **stored(back, ring, mate), **weights(rng, w.astype(BF))}
def setup_inputs_spread(rng):
    d = setup_inputs(rng)
    d["x"] = wide(rng, N, 128, 4 * C, cols=6)
    return d
def check_inputs(d):
    b = []
    for k in ("x", "u", "v"):
        a = np.abs(d[k].astype(np.float32))
        if not (np.isfinite(a).all() and ((a == 0) | (a >= 2.0 ** -30) & (a <= 2.0 ** 30)).all()): b.append("a value of " + k)
    none, least, most = [emit(mx_ref.quantize(np.full((128, 16), k, np.float32).astype(BF)))[1][0, 0] for k in (0.0, 2.0 ** -8, 2.0 ** 8)]
    own = np.arange(C)
    for r in range(N):
        ud, iv, hp, mt = [gentries(d[k][r]) for k in ("ud", "iv", "hp", "mt")]
        if any(((a < 0) | (a >= C)).any() for a in (ud, iv, hp, mt)): b.append("an entry of a list")
        else:
            if (np.sort(ud, axis=1) != own).any(): b.append("ud: a permutation")
            if (take(ud, iv) != own).any(): b.append("iv: the inverse of ud")
            if (take(mt, mt) != own).any() or (mt == own).any(): b.append("mt: pairs of columns")
            at, seen = np.zeros((8, 1), np.int64), np.zeros((8, C), bool)
            for j in range(C):
                at = take(hp, at)
                np.put_along_axis(seen, at, True, axis=1)
            if not seen.all(): b.append("hp: a ring")
        if ((d["wc"][r] == 0x7F) | (d["wc"][r] == 0xFF)).any(): b.append("wc: a code that is no number")
        s = mx_ref.live(d["ws"][r])
        if ((s != none) & ((s < least) | (s > most))).any(): b.append("ws: a scale out of range")
    return b
def halfsum(s, t):
    return ((s.astype(np.float32) + t.astype(np.float32)) * np.float32(0.5)).astype(BF)
def reference(x, u, v, ud, iv, hp, mt, wc, ws):
    qu = [mx_ref.quantize(u[r]) for r in range(N)]
    lay = [pk(wc[r], ws[r]) for r in range(N)]
    to, back, ring, mate = [[gentries(a[r]) for r in range(N)] for a in (ud, iv, hp, mt)]
    now = [x[r] for r in range(N)]
    for step in STEP:
        t, past, sent = [], [], []
        for r in range(N):
            q = mx_ref.quantize(now[r])
            s = mx_ref.matmul(qu[r], q)[::16] > 0
            t.append(decode(q).astype(BF))
            tau = np.where(s & take(s, mate[r]), mate[r], np.arange(C))
            to[r], back[r] = take(to[r], tau), take(tau, back[r])
            e, b = effective(back[r]), ring[r]
            while not take(e, b).all(): b = np.where(take(e, b), b, take(ring[r], b))
            past.append(b)
            sent.append(mx_ref.quantize(halfsum(gcols(t[r], b), gcols(t[r], back[r]))))
        for r in range(N):
            p = r ^ step
            h = tile([mx_ref.matmul(pick(lay[r], np.arange(128 * b, 128 * b + 128)), sent[p]) * np.float32(0.03125) for b in range(4)])
            now[r] = halfsum(gcols(t[r], to[r]), gcols(h, take(past[p], back[r])))
    y, uo = np.zeros((N, 128, C), np.float32), np.zeros((N, 8, C), np.float32)
    oc, osc = np.zeros((N, 128, 4 * C), np.uint8), np.zeros((N, 16, C), np.uint8)
    for r in range(N):
        q = mx_ref.quantize(now[r])
        y[r] = mx_ref.matmul(mx_ref.quantize(v[r]), q)
        uo[r] = to[r]
        oc[r], osc[r] = emit(q)
    return {"y": y, "uo": uo, "oc": oc, "osc": osc}

@@ -1,0 +1,528 @@
+from concourse.mybir import dt, AluOpType, ActivationFunctionType
+
+ALU, ACT = AluOpType, ActivationFunctionType
+
+L = 448
+K = L // 16
+NR = 3
+STEP = [1, 2, 3]
+CUT = 256
+CUTS = {"ring": 0, "w": (0, 14), "b": (0, 14), "c": (0, 14), "r": 14}
+LV = 5
+TW = 464
+
+SCRATCH = {}
+
+
+def _buf(name, cols, dtype="float32", where="sbuf"):
+    SCRATCH[name] = (where, [128, cols], dtype)
+
+
+for _n in ("l_iv", "l_hp", "l_mt"):
+    _buf(_n, K, "int32")
+_buf("x0t", 4 * L, "bfloat16")
+_buf("ut", 512, "bfloat16")
+_buf("vt", 512, "bfloat16")
+_buf("zt", 4 * L, "bfloat16")
+_buf("xnt", 4 * L, "bfloat16")
+_buf("ebuf", 516, "bfloat16")
+for _n, _c in (("uq", 128), ("uqs", 128), ("vq", 128), ("wq", 512), ("eq", 512), ("zq", L)):
+    _buf(_n + "c", _c, "float8_e4m3fn_x4")
+    _buf(_n + "p", _c, "uint8")
+for _m in range(NR + 1):
+    _buf("xqc%d" % _m, L, "float8_e4m3fn_x4")
+    _buf("xqp%d" % _m, L, "uint8")
+for _m in range(NR):
+    _buf("lac%d" % _m, L, "float8_e4m3fn_x4")
+    _buf("lap%d" % _m, L, "uint8")
+    for _n in ("liv", "lbw", "lew", "bw", "ew"):
+        _buf(_n + str(_m), K, "uint16")
+    _buf("udw%d" % _m, K, "uint16")
+    _buf("zo%d" % _m, K, "uint16")
+for _m in range(NR + 1):
+    _buf("ivw%d" % _m, K, "uint16")
+    _buf("mvw%d" % _m, K, "uint16")
+    for _n in ("ivs", "dm"):
+        _buf(_n + str(_m), K)
+_buf("hpw", K, "uint16")
+_buf("mtw", K, "uint16")
+_buf("rw", K, "uint16")
+_buf("pmw", K, "uint16")
+_buf("uoff", 8, "uint16")
+_buf("uoi", 8, "int32")
+_buf("o16", 8, "uint16")
+_buf("ids", 961)
+_buf("w1", 961)
+FS, PS = 968, 456
+WIN = {"f%d" % _k: ("fb", FS * _k) for _k in range(9)}
+for _k, _n in enumerate(("p0", "p1", "p2", "st", "bwin", "mtr")):
+    WIN[_n] = ("wb", PS * _k)
+_buf("fb", 9 * FS)
+_buf("wb", 6 * PS)
+_buf("fw", 8 * K + 32, "uint16")
+_buf("offw", 8 * K, "uint16")
+_buf("sgn", 449, "bfloat16")
+for _n in ("ga", "gb", "ya", "yb", "db"):
+    _buf(_n, L, "bfloat16")
+for _n in ("d2", "sc", "scb", "scm", "scu", "scr", "tmod", "th0", "rrep", "mono", "m1", "vr", "eb", "mv", "ysb", "uf", "s16", "g16"):
+    _buf(_n, L)
+for _n in ("udr", "pmr"):
+    _buf(_n, 449)
+_buf("cidx", K)
+_buf("jws", K)
+_buf("tiny", 12 * K)
+_buf("ti", 4 * K, "int32")
+_buf("pcol", 8, "int32")
+_buf("col", 16)
+_buf("ones", 16)
+_buf("to", 4 * TW, "bfloat16")
+_buf("tp", 4 * TW, "bfloat16")
+_buf("hh", 4 * TW, "bfloat16")
+_buf("g1", 4 * L, "bfloat16")
+_buf("g2", 4 * L, "bfloat16")
+_buf("pa", 2048, "float32", "psum")
+_buf("pb", 2048, "float32", "psum")
+
+LOADS = ["d_hp", "d_iv", "d_mt", "d_u", "d_xa", "d_xb", "d_v", "d_wc", "d_ws"]
+SEMAPHORES = ["sv", "sa", "sp", "sg", "sent", "d_out"] + LOADS + ["%s%d" % (a, m) for a in ("rc", "ri", "rb", "re_") for m in range(NR)]
+SEM = {"V": "sv", "A": "sa", "P": "sp", "G": "sg"}
+CY = 0.00083
+GC = 1.5
+WAKE = 0.06
+DELTA = 0.12
+
+
+def new_prog():
+    return {"ops": [], "wr": {}, "rd": {}}
+
+
+def add(p, eng, fn, r, w, dur, lat=0.0, kind="c", sem=None, val=1):
+    ops = p["ops"]
+    i = len(ops)
+    deps = set()
+    for k in r:
+        if k in p["wr"]:
+            deps.add(p["wr"][k])
+        else:
+            raise ValueError("read before write: " + k)
+    for k in w:
+        if k in p["wr"]:
+            deps.add(p["wr"][k])
+        for j in p["rd"].get(k, ()):
+            deps.add(j)
+    for k in r:
+        p["rd"].setdefault(k, []).append(i)
+    for k in w:
+        p["wr"][k] = i
+        p["rd"][k] = []
+    deps.discard(i)
+    ops.append({"eng": eng, "fn": fn, "deps": sorted(deps), "dur": dur, "lat": lat, "kind": kind, "sem": sem, "val": val})
+    return i
+
+
+def order(ops):
+    n = len(ops)
+    succ = [[] for _ in range(n)]
+    for i, o in enumerate(ops):
+        for d in o["deps"]:
+            succ[d].append(i)
+    prio = [0.0] * n
+    for i in range(n - 1, -1, -1):
+        o = ops[i]
+        prio[i] = o["dur"] + o["lat"] + WAKE + max([prio[s] for s in succ[i]] + [0.0])
+    free, left = {}, [len(o["deps"]) for o in ops]
+    end, when, on = [0.0] * n, [0.0] * n, [None] * n
+    ready = [i for i in range(n) if not left[i]]
+    while ready:
+        cand = []
+        for i in ready:
+            at = max([end[d] + WAKE for d in ops[i]["deps"]] + [0.0])
+            for e in ops[i]["eng"]:
+                cand.append((max(at, free.get(e, 0.0)) if e != "N" else at, i, e))
+        t0 = min(c[0] for c in cand)
+        first = min(c for c in cand if c[0] == t0)
+        eng = [c for c in cand if c[2] == first[2] and c[0] <= t0 + DELTA]
+        t, i, e = max(eng, key=lambda c: (prio[c[1]] - (c[0] - t0), -c[1]))
+        o = ops[i]
+        ready.remove(i)
+        when[i], on[i] = t, e
+        if e != "N":
+            free[e] = t + o["dur"]
+        end[i] = t + o["dur"] + o["lat"]
+        for s in succ[i]:
+            left[s] -= 1
+            if not left[s]:
+                ready.append(s)
+    seq = sorted(range(n), key=lambda i: (when[i], i))
+    return seq, on, max(end), when, end
+
+
+def emit(g, T, p):
+    ops = p["ops"]
+    seq, on, total, when, end = order(ops)
+    q = {"V": g.vector, "A": g.scalar, "P": g.tensor, "G": g, "S": g.sync}
+    count = {e: 0 for e in q}
+    known = {e: {} for e in q}
+    clock = [None] * len(ops)
+    for i in seq:
+        o, e = ops[i], on[i]
+        if e == "N":
+            clock[i] = {o["sem"]: o["val"]}
+            continue
+        need = {}
+        for d in o["deps"]:
+            if ops[d]["kind"] == "r":
+                continue
+            for s, v in clock[d].items():
+                need[s] = max(need.get(s, 0), v)
+        mine = known[e]
+        direct = []
+        for d in sorted(o["deps"], key=lambda d: -when[d]):
+            if ops[d]["kind"] == "r":
+                continue
+            s, v = own(ops, on, clock, d)
+            if mine.get(s, 0) < v:
+                q[e].wait_ge(T.sem[s], v)
+                for s2, v2 in clock[d].items():
+                    if mine.get(s2, 0) < v2:
+                        mine[s2] = v2
+        inst = o["fn"](e)
+        c = dict(mine)
+        if o["kind"] == "c":
+            count[e] += 1
+            inst.then_inc(T.sem[SEM[e]], 1)
+            c[SEM[e]] = count[e]
+        elif o["kind"] == "d":
+            inst.then_inc(T.sem[o["sem"]], 16)
+            c[o["sem"]] = 16
+        clock[i] = c
+        ops[i]["n"] = count[e]
+    return count, known, total
+
+
+def own(ops, on, clock, d):
+    o = ops[d]
+    if o["kind"] == "c":
+        return SEM[on[d]], o["n"]
+    return o["sem"], (16 if o["kind"] == "d" else o["val"])
+
+
+def build(g, core, T, topo):
+    rank = T.rank_of(core)
+    p = new_prog()
+    V, A, P, G = g.vector, g.scalar, g.tensor, g
+    U8, U32 = dt.uint8, dt.uint32
+
+    def v(fn, r, w, el):
+        return add(p, ("V",), lambda e: fn(), r, w, max(64, el) * CY)
+
+    def ts(out, in0, s1, s2, op0, op1, r, w, el):
+        if op1 is None:
+            return v(lambda: V.tensor_scalar(out, in0, s1, None, op0), r, w, el)
+        return v(lambda: V.tensor_scalar(out, in0, s1, s2, op0, op1), r, w, el)
+
+    def tt(out, a, b, op, r, w, el):
+        return v(lambda: V.tensor_tensor(out, a, b, op), r, w, el)
+
+    def fill(ap, c, w, el):
+        return v(lambda: V.memset(ap, c), [], w, el)
+
+    def gat(out, win, off, r, w, el, eng=("V", "A")):
+        def fn(e):
+            if e == "V":
+                return V.tensor_copy(out, win.indirect(off))
+            return A.activation(out, win.indirect(off), ACT.Copy)
+        return add(p, eng, fn, r, w, 0.055 + el * GC * CY)
+
+    def win(n, a, b):
+        t, o = WIN[n]
+        return T[t][:, o + a:o + b]
+
+    def gat2(out, window, off, oo, r, key, cut):
+        h = 16 * cut
+        o = out if cut in (0, K) else None
+        if cut in (0, K):
+            gat(out(0, L), window, off[:, oo:oo + K], r, [key + "a", key + "b"], L, ("A",) if cut == 0 else ("V",))
+            return
+        gat(out(0, h), window, off[:, oo:oo + cut], r, [key + "a"], h, ("V",))
+        gat(out(h, L), window, off[:, oo + cut:oo + K], r, [key + "b"], L - h, ("A",))
+
+    def into(n):
+        return lambda a, b: win(n, 1 + a, 1 + b)
+
+    def ab(k):
+        return [k + "a", k + "b"]
+
+    def relay(src, sc, sck, r, n=L):
+        v(lambda: V.tensor_tensor_scan(sc[:, 0:n], T.d2[:, 0:n], src, 0.0, ALU.mult, ALU.max), r + ["d2"], [sck], n)
+        return sc[:, 15:n:16]
+
+    cp, cpk, pw, thr, kf = [T.col[:, i:i + 1] for i in (0, 1, 2, 3, 4)]
+    bias = [T.col[:, 8 + k:9 + k] for k in range(4)]
+    idc = T.ids[:, 513:961]
+
+    def load(q, out, in_, sem, w, lat, r=()):
+        add(p, (q,), lambda e: (g.sync if e == "S" else g.scalar).dma_start(out, in_), list(r), w, 0.05, lat, "d", sem)
+    load("S", T.l_hp[:], T.hp[:], "d_hp", ["l_hp"], 2.0)
+    load("A", T.l_iv[:], T.iv[:], "d_iv", ["l_iv"], 2.0)
+    load("A", T.l_mt[:], T.mt[:], "d_mt", ["l_mt"], 2.0)
+    load("S", T.ut[:], T.u[:], "d_u", ["ut"], 2.5)
+    load("S", T.x0t[:, 0:4 * CUT], T.x[:, 0:4 * CUT], "d_xa", ["x0a"], 3.5)
+    load("S", T.x0t[:, 4 * CUT:4 * L], T.x[:, 4 * CUT:4 * L], "d_xb", ["x0b"], 4.0)
+    load("S", T.wqc[:].bitcast(U8), T.wc[:], "d_wc", ["wqc"], 4.0, ["x0b"])
+    load("S", T.wqp[:], T.ws[:], "d_ws", ["wqp"], 3.0, ["x0b"])
+    load("S", T.vt[:], T.v[:], "d_v", ["vt"], 3.0, ["x0b"])
+
+    def iota(out, pat, base, cm, w, el, flag=True):
+        if flag:
+            fn = lambda e: G.iota(out, pat, base, cm, allow_small_or_imprecise_dtypes=True)
+        else:
+            fn = lambda e: G.iota(out, pat, base, cm)
+        add(p, ("G",), fn, [], w, 0.13 + 2 * el * CY)
+    iota(T.pcol[:, 0:1], [[0, 1]], 0, 1, ["pcol"], 1, False)
+    iota(T.tmod[:], [[0, K], [1, 16]], 0, 0, ["tmod"], L)
+    iota(idc, [[1, L]], 513, 0, ["idc"], L)
+    iota(T.cidx[:], [[16, K]], 1, 0, ["cidx"], K)
+    iota(T.uoi[:], [[16, 8]], 0, 0, ["uoi"], 8, False)
+    for k in range(4):
+        iota(win("f%d" % k, 449, 961), [[1, 512]], 449, 0, ["f%dI" % k], 512)
+    fill(T.ebuf[:], 0.5, ["ebuf0"], 258)
+    add(p, ("G",), lambda e: G.affine_select(T.ebuf[:], T.ebuf[:], [[-1, 516]], ALU.is_equal, 0.0, 3, 4), ["ebuf0"], ["ebuf"], 0.17 + 2 * 516 * CY)
+    fill(T.ones[:], 1.0, ["ones"], 16)
+    ts(T.pcol[:, 1:2], T.pcol[:, 0:1], 15, None, ALU.bitwise_and, None, ["pcol"], ["kint"], 1)
+    v(lambda: V.tensor_copy(kf, T.pcol[:, 1:2]), ["kint"], ["kf"], 1)
+    ts(T.d2[:], T.tmod[:], kf, 2.0, ALU.is_gt, ALU.mult, ["tmod", "kf"], ["d2"], L)
+    relay(T.ones[:], T.s16, "s16", ["ones"], 16)
+    v(lambda: V.tensor_copy(pw, T.s16[:, 15:16]), ["s16"], ["pw"], 1)
+    v(lambda: V.reciprocal(cp, pw), ["pw"], ["cp"], 300)
+    ts(cpk, cp, 1.0 / 512, None, ALU.mult, None, ["cp"], ["cpk"], 1)
+    tt(T.col[:, 5:6], pw, pw, ALU.mult, ["pw"], ["pw2"], 1)
+    ts(thr, T.col[:, 5:6], 4.0, None, ALU.mult, None, ["pw2"], ["thr"], 1)
+    for k in range(4):
+        ts(T.pcol[:, 2 + k:3 + k], T.pcol[:, 0:1], 1 << k, None, ALU.bitwise_and, None, ["pcol"], ["bit%d" % k], 1)
+        if k:
+            ts(bias[k], T.pcol[:, 2 + k:3 + k], -512.0 / (1 << k), None, ALU.mult, None, ["bit%d" % k], ["bias%d" % k], 1)
+        else:
+            ts(T.o16[:, 0:1], T.pcol[:, 2:3], -512.0, 960.0, ALU.mult, ALU.add, ["bit0"], ["o16_0"], 1)
+    fill(T.ids[:, 0:512], 512.0, ["idl"], 512)
+    fill(T.ids[:, 512:513], 960.0, ["idz"], 1)
+    fill(T.fb[:, 0:8 * FS + 1:FS], 512.0, ["f%di" % k for k in range(9)], 9)
+    fill(T.wb[:, 0:5 * PS + 1:PS], 512.0, ["p0i", "p1i", "p2i", "sti", "bwini", "mtri"], 6)
+    fill(T.wb[:, 449:449 + 2 * PS + 1:PS], 961.0, ["p0j", "p1j", "p2j"], 3)
+    fill(T.sgn[:, 0:1], 1.0, ["sgni"], 1)
+    fill(T.w1[:, 0:513], 961.0, ["w1i"], 513)
+    for n in ("to", "tp", "hh"):
+        fill(T[n][:, 0:3 * TW + 1:TW], 0.0, ["%si%d" % (n, b) for b in range(4)], 4)
+    ts(T.db[:], T.tmod[:], kf, 2.0, ALU.is_gt, ALU.mult, ["tmod", "kf"], ["db"], L)
+    ts(T.jws[:], T.cidx[:], kf, 1.0 / 512, ALU.add, ALU.mult, ["cidx", "kf"], ["jws"], K)
+    ts(T.th0[:], idc, 0.5, 255.0, ALU.mult, ALU.add, ["idc"], ["th0"], L)
+    v(lambda: V.tensor_copy(T.uoff[:], T.uoi[:]), ["uoi"], ["uoff"], 8)
+
+    ts(T.hpw[:], T.l_hp[:], 1.0, None, ALU.add, None, ["l_hp"], ["hpw"], K)
+    ts(T.ivw0[:], T.l_iv[:], 1.0, None, ALU.add, None, ["l_iv"], ["ivw0"], K)
+    ts(T.ivs0[:], T.l_iv[:], 1.0 / 512, 1.0 / 512, ALU.mult, ALU.add, ["l_iv"], ["ivs0"], K)
+    ts(T.mtw[:], T.l_mt[:], 1.0, None, ALU.add, None, ["l_mt"], ["mtw"], K)
+
+    v(lambda: V.quantize_mx(T.uqc[:, 0:128], T.uqp[:, 0:128], T.ut[:]), ["ut"], ["uq"], 140)
+    v(lambda: V.tensor_copy(T.uqsc[:, 0:128].bitcast(U32), T.uqc[:, 0:128].bitcast(U32).indirect(T.uoff[:, 0:8])), ["uq", "uoff"], ["uqsc"], 200)
+    v(lambda: V.tensor_copy(T.uqsp[:, 0:128], T.uqp[:, 0:128].indirect(T.uoff[:, 0:8])), ["uq", "uoff"], ["uqsp"], 200)
+    for h, (a, b) in enumerate(((0, CUT), (CUT, L))):
+        v(lambda a=a, b=b: V.quantize_mx(T.xqc0[:, a:b], T.xqp0[:, a:b], T.x0t[:, 4 * a:4 * b]), ["x0" + "ab"[h]], ["xq0" + "ab"[h]], (b - a) * 1.06 + 14)
+    for b in range(4):
+        v(lambda b=b: V.quantize_mx(T.eqc[:, 128 * b:128 * b + 128], T.eqp[:, 128 * b:128 * b + 128], T.ebuf[:, 3 - b:515 - b]), ["ebuf"], ["eq%d" % b], 150)
+
+    def send(dst, out, in_, sem, r, w, lat, key):
+        rid, pid = topo.addr(dst)[:2]
+        add(p, ("G",), lambda e: g.remote_dma(out, in_, T.sem[sem], T.sem.sent, pid, rid, topo.mask(core, dst)), r, [key], 0.3, 0.0, "r")
+        sent[0] += len(topo.engines(core, dst))
+
+    sent = [0]
+
+    def arrive(sem, val, r, w, lat):
+        add(p, ("N",), None, r, w, 0.0, lat, "n", sem, val)
+
+    def ring_ops():
+        v(lambda: V.tensor_copy(win("f0", 0, 449).indirect(T.hpw[:, 0:K]), idc), ["hpw", "idc", "f0i"], ab("f0"), L * 3)
+        for k in range(9):
+            fk = win("f%d" % k, 0, 449)
+            if k < 8:
+                s = relay(win("f%d" % k, 1, 449), T.scr, "scr", ab("f%d" % k))
+                ts(T.fw[:, K * k:K * k + K], s, cp, -512.0, ALU.mult, ALU.add, ["scr", "cp"], ["fw%d" % k], K)
+            r0 = ab("f%d" % k) + ["f%di" % k]
+            if k < 4:
+                o = T.rrep[:, 0:16] if k == 3 else T.g16[:, 16 * k:16 * k + 16]
+                gat(o, win("f%d" % k, 0, 961), T.o16[:, 2 * k:2 * k + 1], r0 + ["f%dI" % k, "o16_%d" % k], ["r16_%d" % k], 32, ("V",))
+                s = relay(o, T.s16, "s16", ["r16_%d" % k], 16)
+                if k < 3:
+                    ts(T.o16[:, 2 * k + 2:2 * k + 3], s, cp, bias[k + 1], ALU.mult, ALU.add, ["s16", "cp", "bias%d" % (k + 1)], ["o16_%d" % (k + 1)], 1)
+                else:
+                    ts(T.rw[:, 0:1], s, cp, -512.0, ALU.mult, ALU.add, ["s16", "cp"], ["rw0"], 1)
+            else:
+                b = 1 << (k - 4)
+                n = min(b, K - b)
+                gat(T.rrep[:, 16 * b:16 * b + 16 * n], fk, T.rw[:, 0:n], r0 + ["rw%d" % j for j in range(k - 3)], ["r16_%d" % k], 16 * n)
+                s = relay(T.rrep[:, 16 * b:16 * b + 16 * n], T.s16, "s16", ["r16_%d" % k], 16 * n)
+                ts(T.rw[:, b:b + n], s, cp, -512.0, ALU.mult, ALU.add, ["s16", "cp"], ["rw%d" % (k - 3)], n)
+            if k < 8:
+                gat2(into("f%d" % (k + 1)), fk, T.fw, K * k, r0 + ["fw%d" % k], "f%d" % (k + 1), CUTS["ring"])
+        rws = ["rw%d" % j for j in range(6)]
+        v(lambda: V.tensor_copy(T.pmr[:, 0:449].indirect(T.rw[:, 0:K]), T.ids[:, 512:960]), rws + ["idz", "idc"], ["pmr"], L * 3)
+        s = relay(T.pmr[:, 1:449], T.scr, "scr", ["pmr"])
+        ts(T.pmw[:], s, cp, -512.0, ALU.mult, ALU.add, ["scr", "cp"], ["pmw"], K)
+        ts(T.m1[:], T.rrep[:], 1.0 / 1024, None, ALU.mult, None, ["r16_%d" % k for k in range(3, 9)], ["m1"], L)
+        tt(T.mono[:], T.m1[:], T.th0[:], ALU.add, ["m1", "th0"], ["mono"], 2 * L)
+
+    gat2(into("mtr"), T.ids[:, 512:961], T.mtw, 0, ["mtw", "idc", "idz"], "mtr", 0)
+    RW = ["rw%d" % j for j in range(6)]
+
+    def mates_of(m):
+        gat2(lambda a, b: T.mv[:, a:b], win("mtr", 0, 449), T["ivw%d" % m], 0, ab("mtr") + ["mtri", "ivw%d" % m], "mv", 0)
+        s = relay(T.mv[:], T.scm, "scm", ab("mv"))
+        ts(T["mvw%d" % m][:], s, cp, -512.0, ALU.mult, ALU.add, ["scm", "cp"], ["mvw%d" % m], K)
+        ts(T.tiny[:, 0:K], s, cpk, -1.0, ALU.mult, ALU.add, ["scm", "cpk"], ["mvs"], K)
+        tt(T["dm%d" % m][:], T.tiny[:, 0:K], T["ivs%d" % m][:], ALU.subtract, ["mvs", "ivs%d" % m], ["dm%d" % m], 64)
+
+    def places(sc, sck, out, key, i):
+        t = T.ti
+        ts(t[:, 2 * K * i:2 * K * i + K], sc[:, 15:L:16], cp, 1024.0, ALU.mult, ALU.mult, [sck, "cp"], ["ti%da" % i], K)
+        ts(t[:, 2 * K * i + K:2 * K * i + 2 * K], t[:, 2 * K * i:2 * K * i + K], 511, None, ALU.bitwise_and, None, ["ti%da" % i], ["ti%db" % i], K)
+        v(lambda: V.tensor_copy(out[:], t[:, 2 * K * i + K:2 * K * i + 2 * K]), ["ti%db" % i], [key], K)
+
+    def bank(i):
+        t = (T.pa, T.pb)[i // 4]
+        return t, 512 * (i % 4)
+
+    def mm(i, wc, wp, a, xc, xp, c0, c1, r):
+        t, o = bank(i)
+        add(p, ("P",), lambda e: P.matmul_mx(t[:, o:o + c1 - c0], wc[:, a:a + 128], wp[:, a:a + 128], xc[:, c0:c1], xp[:, c0:c1], True, True),
+            r, ["bank%d" % i], (c1 - c0 + 16) * CY)
+
+    def unload(i, out, n, scale, w):
+        t, o = bank(i)
+
+        def fn(e):
+            if e == "A":
+                return A.activation(out, t[:, o:o + n], ACT.Copy) if scale == 1.0 else A.activation(out, t[:, o:o + n], ACT.Copy, scale=scale)
+            return V.tensor_copy(out, t[:, o:o + n]) if scale == 1.0 else V.tensor_scalar(out, t[:, o:o + n], scale, None, ALU.mult)
+        add(p, ("V", "A"), fn, [], ["bank%d" % i] + w, 0.02 + n * CY)
+
+    mates_of(0)
+    for m in range(NR):
+        dst = T.cores[rank ^ STEP[m]]
+        n8 = len(topo.engines(core, dst))
+        X = ["xq%da" % m, "xq%db" % m]
+        xc, xp, lc, lp = T["xqc%d" % m], T["xqp%d" % m], T["lac%d" % m], T["lap%d" % m]
+        nx = m + 1
+        send(dst, lc[:].bitcast(U8), xc[:].bitcast(U8), "rc%d" % m, X, [], 0, "out_c%d" % m)
+        send(dst, lp[:], xp[:], "rc%d" % m, X, [], 0, "out_s%d" % m)
+        arrive("rc%d" % m, 2 * n8, ["out_c%d" % m, "out_s%d" % m], ["la%d" % m], 6.0)
+        mm(4, T.uqsc, T.uqsp, 0, xc, xp, 0, L, X + ["uqsc", "uqsp"])
+        ts(T.sgn[:, 1:449], T.pb[:, 0:L], 0.0, 1.0, ALU.is_gt, ALU.add, [], ["bank4", "sgn"], L)
+        gat(T.ga[:], T.sgn[:, 0:449], T["ivw%d" % m][:, 0:K], ["sgn", "sgni", "ivw%d" % m], ["ga"], L, ("V",))
+        gat(T.gb[:], T.sgn[:, 0:449], T["mvw%d" % m][:, 0:K], ["sgn", "sgni", "mvw%d" % m], ["gb"], L, ("A",))
+        for a in "ab":
+            v(lambda a=a: V.tensor_tensor_scan(T["y" + a][:], T.db[:], T["g" + a][:], 0.0, ALU.mult, ALU.max), ["db", "g" + a], ["y" + a], L // 2)
+        tn = [T.tiny[:, K * i:K * i + K] for i in range(12)]
+        tt(tn[1], T.ya[:, 15:L:16], T.yb[:, 15:L:16], ALU.mult, ["ya", "yb"], ["t1"], 64)
+        ts(tn[2], tn[1], thr, None, ALU.is_ge, None, ["t1", "thr"], ["t2"], K)
+        tt(tn[3], tn[2], T["dm%d" % m][:], ALU.mult, ["t2", "dm%d" % m], ["t3"], 64)
+        tt(T["ivs%d" % nx][:], tn[3], T["ivs%d" % m][:], ALU.add, ["t3", "ivs%d" % m], ["ivs%d" % nx], 64)
+        tt(tn[4], T["ivs%d" % nx][:], T.jws[:], ALU.is_gt, ["ivs%d" % nx, "jws"], ["t4"], 64)
+        tt(tn[5], tn[4], T["ivs%d" % nx][:], ALU.add, ["t4", "ivs%d" % nx], ["t5"], 64)
+        zo = T["zo%d" % m]
+        ts(zo[:], tn[5], 512.0, None, ALU.mult, None, ["t5"], ["zo%d" % m], K)
+        ivw = T["ivw%d" % nx]
+        ts(ivw[:], T["ivs%d" % nx][:], 512.0, None, ALU.mult, None, ["ivs%d" % nx], ["ivw%d" % nx], K)
+        send(dst, T["liv%d" % m][:], ivw[:], "ri%d" % m, ["ivw%d" % nx], [], 0, "out_i%d" % m)
+        arrive("ri%d" % m, n8, ["out_i%d" % m], ["liv%d" % m], 2.0)
+        first = min(m, 1)
+        gat2(lambda a, b: T.w1[:, 513 + a:513 + b], T.ids[:, 0:961], zo, 0, ["idl", "idz", "idc", "zo%d" % m], "w1", CUTS["w"][first])
+        gat2(into("p0"), T.w1[:, 0:961], zo, 0, ab("w1") + ["w1i", "zo%d" % m], "p0", CUTS["w"][first])
+        a, b, c = 0, 1, 2
+        for lv in range(LV):
+            A_, B_, C_ = ["p%d" % i for i in (a, b, c)]
+            o = K * lv
+            s = relay(win(A_, 1, 449), T.sc, "sc", ab(A_))
+            ts(T.offw[:, o:o + K], s, cp, -512.0, ALU.mult, ALU.add, ["sc", "cp"], ["offw%d" % lv], K)
+            gat2(into(B_), win(A_, 0, 450), T.offw, o, ab(A_) + [A_ + "i", A_ + "j", "offw%d" % lv], B_, CUTS["b"][first])
+            gat2(into(C_), win(B_, 0, 450), T.offw, o, ab(B_) + [B_ + "i", B_ + "j", "offw%d" % lv], C_, CUTS["c"][first])
+            a, c = c, a
+        A_ = "p%d" % a
+        if m == 0:
+            ring_ops()
+        gat2(lambda a, b: T.vr[:, a:b], win(A_, 0, 450), T.rw, 0, ab(A_) + [A_ + "i", A_ + "j"] + RW, "vr", CUTS["r"])
+        v(lambda: V.tensor_tensor_scan(win("st", 1, 449), T.vr[:], T.mono[:], 512.0, ALU.max, ALU.min), ab("vr") + ["mono"], ["st"], L)
+        gat2(into("bwin"), win("st", 0, 449), T.pmw, 0, ["st", "sti", "pmw"], "bwin", CUTS["r"])
+        relay(win("bwin", 1, 449), T.sc, "sc", ab("bwin"))
+        places(T.sc, "sc", T["bw%d" % m], "bw%d" % m, 0)
+        send(dst, T["lbw%d" % m][:], T["bw%d" % m][:], "rb%d" % m, ["bw%d" % m], [], 0, "out_b%d" % m)
+        arrive("rb%d" % m, n8, ["out_b%d" % m], ["lbw%d" % m], 2.0)
+        gat2(lambda a, b: T.eb[:, a:b], win("bwin", 0, 449), T["liv%d" % m], 0, ab("bwin") + ["bwini", "liv%d" % m], "eb", 0)
+        relay(T.eb[:], T.scb, "scb", ab("eb"))
+        places(T.scb, "scb", T["ew%d" % m], "ew%d" % m, 1)
+        send(dst, T["lew%d" % m][:], T["ew%d" % m][:], "re_%d" % m, ["ew%d" % m], [], 0, "out_e%d" % m)
+        arrive("re_%d" % m, n8, ["out_e%d" % m], ["lew%d" % m], 2.0)
+        for b in range(4):
+            mm(b, T.eqc, T.eqp, 128 * b, xc, xp, 0, L, X + ["eq%d" % b])
+            unload(b, T.to[:, TW * b + 1:TW * b + 449], L, 1.0, ["to%d" % b])
+        for b in range(4):
+            mm(4 + b, T.eqc, T.eqp, 128 * b, lc, lp, 0, L, ["la%d" % m, "eq%d" % b])
+            unload(4 + b, T.tp[:, TW * b + 1:TW * b + 449], L, 1.0, ["tp%d" % b])
+        for b in range(4):
+            gat(T.g1[:, L * b:L * b + L], T.tp[:, TW * b:TW * b + 449], T["liv%d" % m][:, 0:K], ["tp%d" % b, "tpi%d" % b, "liv%d" % m], ["g1%d" % b], L)
+        v(lambda ivw=ivw: V.tensor_copy(T.udr[:, 0:449].indirect(ivw[:, 0:K]), idc), ["ivw%d" % nx, "idc"], ["udr"], L * 3)
+        s = relay(T.udr[:, 1:449], T.scu, "scu", ["udr"])
+        ts(T["udw%d" % m][:], s, cp, -512.0, ALU.mult, ALU.add, ["scu", "cp"], ["udw%d" % m], K)
+        for b in range(4):
+            gat(T.g2[:, L * b:L * b + L], T.to[:, TW * b:TW * b + 449], T["udw%d" % m][:, 0:K], ["to%d" % b, "toi%d" % b, "udw%d" % m], ["g2%d" % b], L)
+        for h, (c0, c1) in enumerate(((0, CUT), (CUT, L))):
+            for b in range(4):
+                v(lambda b=b, c0=c0, c1=c1, m=m: V.tensor_tensor(T.zt[:, 4 * c0 + b:4 * c1:4], T.tp[:, TW * b:TW * b + 449].indirect(T["lbw%d" % m][:, c0 // 16:c1 // 16]),
+                                                                 T.g1[:, L * b + c0:L * b + c1], ALU.add),
+                  ["tp%d" % b, "tpi%d" % b, "lbw%d" % m, "g1%d" % b], ["zt%d%d" % (h, b)], 60 + (c1 - c0) * GC)
+            v(lambda c0=c0, c1=c1: V.quantize_mx(T.zqc[:, c0:c1], T.zqp[:, c0:c1], T.zt[:, 4 * c0:4 * c1]), ["zt%d%d" % (h, b) for b in range(4)], ["zq%d" % h], 14 + (c1 - c0) * 1.06)
+            for b in range(4):
+                i = 4 * h + b
+                mm(i, T.wqc, T.wqp, 128 * b, T.zqc, T.zqp, c0, c1, ["wqc", "wqp", "zq%d" % h])
+                unload(i, T.hh[:, TW * b + 1 + c0:TW * b + 1 + c1], c1 - c0, 0.015625, ["hh%d%d" % (b, h)])
+        for b in range(4):
+            v(lambda b=b, m=m: V.tensor_tensor(T.xnt[:, b:4 * L:4], T.hh[:, TW * b:TW * b + 449].indirect(T["lew%d" % m][:, 0:K]), T.g2[:, L * b:L * b + L], ALU.add),
+              ["hh%d0" % b, "hh%d1" % b, "hhi%d" % b, "lew%d" % m, "g2%d" % b], ["xnt%d" % b], 60 + L * GC)
+        v(lambda nx=nx: V.quantize_mx(T["xqc%d" % nx][:], T["xqp%d" % nx][:], T.xnt[:]), ["xnt%d" % b for b in range(4)], ["xq%da" % nx, "xq%db" % nx], 14 + L * 1.06)
+        if nx < NR:
+            mates_of(nx)
+
+    outs = [0]
+
+    def store(q, out, in_, r):
+        outs[0] += 16
+        add(p, (q,), lambda e: (g.sync if e == "S" else g.scalar).dma_start(out, in_), r, ["st%d" % outs[0]], 0.05, 2.0, "d", "d_out")
+    X = ["xq3a", "xq3b"]
+    ts(T.uf[:], T.udr[:, 1:449], -513.0, None, ALU.add, None, ["udr"], ["uf"], L)
+    store("S", T.uo[:], T.uf[0:128:16, :], ["uf"])
+    v(lambda: V.quantize_mx(T.vqc[:], T.vqp[:], T.vt[:]), ["vt"], ["vq"], 140)
+    mm(4, T.vqc, T.vqp, 0, T.xqc3, T.xqp3, 0, L, X + ["vq"])
+    unload(4, T.ysb[:], L, 1.0, ["ysb"])
+    store("S", T.oc[:], T.xqc3[:].bitcast(U8), X)
+    for k in range(4):
+        store("AS"[k % 2], T.osc[4 * k:4 * k + 4, 0:L], T.xqp3[32 * k:32 * k + 4, 0:L], X)
+    store("A", T.y[:], T.ysb[:], ["ysb"])
+    return p, sent, outs, n8
+
+
+def rank_program(g, core, T, topo):
+    rank = T.rank_of(core)
+    if rank is None:
+        return
+    p, sent, outs, n8 = build(g, core, T, topo)
+    count, known, total = emit(g, T, p)
+    for e, s in SEM.items():
+        if count[e]:
+            g.wait_ge(T.sem[s], count[e])
+    for s in LOADS:
+        g.wait_ge(T.sem[s], 16)
+    g.wait_ge(T.sem.d_out, outs[0])
+    for m in range(NR):
+        for a, k in (("rc", 2), ("ri", 1), ("rb", 1), ("re_", 1)):
+            g.wait_ge(T.sem["%s%d" % (a, m)], k * n8)
+    g.wait_ge(T.sem.sent, sent[0])

@@ -1,3 +1,4 @@
+import numpy as np
 from concourse.mybir import dt, AluOpType, ActivationFunctionType
 
 ALU, ACT = AluOpType, ActivationFunctionType
@@ -7,7 +8,7 @@ K = L // 16
 NR = 3
 STEP = [1, 2, 3]
 CUT = 256
-CUTS = {"ring": 0, "w": (0, 14), "b": (0, 14), "c": (0, 14), "r": 14}
+CUTS = {"ring": 0, "w": (0, 12), "b": (0, 14), "c": (0, 12), "r": 12}
 LV = 5
 TW = 464
 
@@ -18,7 +19,7 @@ def _buf(name, cols, dtype="float32", where="sbuf"):
     SCRATCH[name] = (where, [128, cols], dtype)
 
 
-for _n in ("l_iv", "l_hp", "l_mt"):
+for _n in ("l_iv", "l_hp", "l_mt", "l_ud"):
     _buf(_n, K, "int32")
 _buf("x0t", 4 * L, "bfloat16")
 _buf("ut", 512, "bfloat16")
@@ -42,35 +43,35 @@ for _m in range(NR):
 for _m in range(NR + 1):
     _buf("ivw%d" % _m, K, "uint16")
     _buf("mvw%d" % _m, K, "uint16")
-    for _n in ("ivs", "dm"):
-        _buf(_n + str(_m), K)
+FLOATS = [_n + str(_m) for _m in range(NR + 1) for _n in ("ivs", "dm", "z", "dz", "uds", "dmu")]
+_buf("lst", K * len(FLOATS))
+_buf("udwi", K, "uint16")
 _buf("hpw", K, "uint16")
 _buf("mtw", K, "uint16")
 _buf("rw", K, "uint16")
 _buf("pmw", K, "uint16")
 _buf("uoff", 8, "uint16")
 _buf("uoi", 8, "int32")
-_buf("o16", 8, "uint16")
+_buf("o16", 16, "uint16")
 _buf("ids", 961)
 _buf("w1", 961)
 FS, PS = 968, 456
 WIN = {"f%d" % _k: ("fb", FS * _k) for _k in range(9)}
-for _k, _n in enumerate(("p0", "p1", "p2", "st", "bwin", "mtr")):
+for _k, _n in enumerate(("p0", "p1", "p2", "st", "bwin", "mtr", "udrep")):
     WIN[_n] = ("wb", PS * _k)
 _buf("fb", 9 * FS)
-_buf("wb", 6 * PS)
+_buf("wb", 7 * PS)
 _buf("fw", 8 * K + 32, "uint16")
 _buf("offw", 8 * K, "uint16")
 _buf("sgn", 449, "bfloat16")
-for _n in ("ga", "gb", "ya", "yb", "db"):
+for _n in ("ga", "gb", "gm", "ya", "yb", "yc", "yd", "db"):
     _buf(_n, L, "bfloat16")
-for _n in ("d2", "sc", "scb", "scm", "scu", "scr", "tmod", "th0", "rrep", "mono", "m1", "vr", "eb", "mv", "ysb", "uf", "s16", "g16"):
+for _n in ("d2", "sc", "scb", "scm", "scu", "scr", "tmod", "th0", "rrep", "mono", "m1", "vr", "eb", "mv", "um", "ysb", "uf", "uf0", "s16", "g16"):
     _buf(_n, L)
-for _n in ("udr", "pmr"):
-    _buf(_n, 449)
+_buf("pmr", 449)
 _buf("cidx", K)
 _buf("jws", K)
-_buf("tiny", 12 * K)
+_buf("tiny", 15 * K)
 _buf("ti", 4 * K, "int32")
 _buf("pcol", 8, "int32")
 _buf("col", 16)
@@ -83,13 +84,16 @@ _buf("g2", 4 * L, "bfloat16")
 _buf("pa", 2048, "float32", "psum")
 _buf("pb", 2048, "float32", "psum")
 
-LOADS = ["d_hp", "d_iv", "d_mt", "d_u", "d_xa", "d_xb", "d_v", "d_wc", "d_ws"]
+LOADS = ["d_hp", "d_iv", "d_mt", "d_ud", "d_u", "d_xa", "d_xb", "d_v", "d_wc", "d_ws"]
 SEMAPHORES = ["sv", "sa", "sp", "sg", "sent", "d_out"] + LOADS + ["%s%d" % (a, m) for a in ("rc", "ri", "rb", "re_") for m in range(NR)]
 SEM = {"V": "sv", "A": "sa", "P": "sp", "G": "sg"}
 CY = 0.00083
 GC = 1.5
-WAKE = 0.06
+WAKE = 0.08
 DELTA = 0.12
+AHEAD = 0.8
+G1 = ("A",)
+SPLIT = True
 
 
 def new_prog():
@@ -120,8 +124,22 @@ def add(p, eng, fn, r, w, dur, lat=0.0, kind="c", sem=None, val=1):
     return i
 
 
+TRIES = 24
+NOISE = 0.6
+
+
 def order(ops):
+    best = None
+    for k in range(TRIES):
+        s = schedule(ops, k)
+        if best is None or s[2] < best[2]:
+            best = s
+    return best
+
+
+def schedule(ops, seed):
     n = len(ops)
+    rng = np.random.RandomState(seed)
     succ = [[] for _ in range(n)]
     for i, o in enumerate(ops):
         for d in o["deps"]:
@@ -130,6 +148,8 @@ def order(ops):
     for i in range(n - 1, -1, -1):
         o = ops[i]
         prio[i] = o["dur"] + o["lat"] + WAKE + max([prio[s] for s in succ[i]] + [0.0])
+    if seed:
+        prio = [a + NOISE * float(b) for a, b in zip(prio, rng.standard_normal(n))]
     free, left = {}, [len(o["deps"]) for o in ops]
     end, when, on = [0.0] * n, [0.0] * n, [None] * n
     ready = [i for i in range(n) if not left[i]]
@@ -141,7 +161,7 @@ def order(ops):
                 cand.append((max(at, free.get(e, 0.0)) if e != "N" else at, i, e))
         t0 = min(c[0] for c in cand)
         first = min(c for c in cand if c[0] == t0)
-        eng = [c for c in cand if c[2] == first[2] and c[0] <= t0 + DELTA]
+        eng = [c for c in cand if c[2] == first[2] and c[0] <= t0 + max(DELTA, AHEAD * ops[first[1]]["dur"])]
         t, i, e = max(eng, key=lambda c: (prio[c[1]] - (c[0] - t0), -c[1]))
         o = ops[i]
         ready.remove(i)
@@ -257,15 +277,25 @@ def build(g, core, T, topo):
         v(lambda: V.tensor_tensor_scan(sc[:, 0:n], T.d2[:, 0:n], src, 0.0, ALU.mult, ALU.max), r + ["d2"], [sck], n)
         return sc[:, 15:n:16]
 
+    def relay2(key, sck, cut):
+        h = 16 * cut
+        if cut in (0, K):
+            return relay(win(key, 1, 1 + L), T.sc, sck + "b", ab(key)), [sck + "b"]
+        for a, b, c in ((0, h, "a"), (h, L, "b")):
+            v(lambda a=a, b=b: V.tensor_tensor_scan(T.sc[:, a:b], T.d2[:, a:b], win(key, 1 + a, 1 + b), 0.0, ALU.mult, ALU.max), [key + c, "d2"], [sck + c], b - a)
+        return T.sc[:, 15:L:16], ab(sck)
+
     cp, cpk, pw, thr, kf = [T.col[:, i:i + 1] for i in (0, 1, 2, 3, 4)]
     bias = [T.col[:, 8 + k:9 + k] for k in range(4)]
     idc = T.ids[:, 513:961]
+    fl = {n: T.lst[:, K * i:K * i + K] for i, n in enumerate(FLOATS)}
 
     def load(q, out, in_, sem, w, lat, r=()):
         add(p, (q,), lambda e: (g.sync if e == "S" else g.scalar).dma_start(out, in_), list(r), w, 0.05, lat, "d", sem)
     load("S", T.l_hp[:], T.hp[:], "d_hp", ["l_hp"], 2.0)
     load("A", T.l_iv[:], T.iv[:], "d_iv", ["l_iv"], 2.0)
     load("A", T.l_mt[:], T.mt[:], "d_mt", ["l_mt"], 2.0)
+    load("A", T.l_ud[:], T.ud[:], "d_ud", ["l_ud"], 2.0)
     load("S", T.ut[:], T.u[:], "d_u", ["ut"], 2.5)
     load("S", T.x0t[:, 0:4 * CUT], T.x[:, 0:4 * CUT], "d_xa", ["x0a"], 3.5)
     load("S", T.x0t[:, 4 * CUT:4 * L], T.x[:, 4 * CUT:4 * L], "d_xb", ["x0b"], 4.0)
@@ -300,32 +330,33 @@ def build(g, core, T, topo):
     ts(thr, T.col[:, 5:6], 4.0, None, ALU.mult, None, ["pw2"], ["thr"], 1)
     for k in range(4):
         ts(T.pcol[:, 2 + k:3 + k], T.pcol[:, 0:1], 1 << k, None, ALU.bitwise_and, None, ["pcol"], ["bit%d" % k], 1)
-        if k:
-            ts(bias[k], T.pcol[:, 2 + k:3 + k], -512.0 / (1 << k), None, ALU.mult, None, ["bit%d" % k], ["bias%d" % k], 1)
-        else:
-            ts(T.o16[:, 0:1], T.pcol[:, 2:3], -512.0, 960.0, ALU.mult, ALU.add, ["bit0"], ["o16_0"], 1)
+        ts(bias[k], T.pcol[:, 2 + k:3 + k], 512.0 / (1 << k), -512.0, ALU.mult, ALU.add, ["bit%d" % k], ["bias%d" % k], 1)
+    fill(T.o16[:, 8:9], 448, ["o16_s"], 1)
     fill(T.ids[:, 0:512], 512.0, ["idl"], 512)
     fill(T.ids[:, 512:513], 960.0, ["idz"], 1)
     fill(T.fb[:, 0:8 * FS + 1:FS], 512.0, ["f%di" % k for k in range(9)], 9)
-    fill(T.wb[:, 0:5 * PS + 1:PS], 512.0, ["p0i", "p1i", "p2i", "sti", "bwini", "mtri"], 6)
+    fill(T.wb[:, 0:6 * PS + 1:PS], 512.0, ["p0i", "p1i", "p2i", "sti", "bwini", "mtri", "udrepi"], 7)
     fill(T.wb[:, 449:449 + 2 * PS + 1:PS], 961.0, ["p0j", "p1j", "p2j"], 3)
     fill(T.sgn[:, 0:1], 1.0, ["sgni"], 1)
     fill(T.w1[:, 0:513], 961.0, ["w1i"], 513)
     for n in ("to", "tp", "hh"):
         fill(T[n][:, 0:3 * TW + 1:TW], 0.0, ["%si%d" % (n, b) for b in range(4)], 4)
-    ts(T.db[:], T.tmod[:], kf, 2.0, ALU.is_gt, ALU.mult, ["tmod", "kf"], ["db"], L)
+    add(p, ("A",), lambda e: A.activation(T.db[:], T.d2[:], ACT.Copy), ["d2"], ["db"], L * CY)
     ts(T.jws[:], T.cidx[:], kf, 1.0 / 512, ALU.add, ALU.mult, ["cidx", "kf"], ["jws"], K)
-    ts(T.th0[:], idc, 0.5, 255.0, ALU.mult, ALU.add, ["idc"], ["th0"], L)
+    add(p, ("V", "A"), lambda e: V.tensor_scalar(T.th0[:], idc, 0.5, 255.0, ALU.mult, ALU.add) if e == "V" else
+        A.activation(T.th0[:], idc, ACT.Copy, bias=255.0, scale=0.5), ["idc"], ["th0"], L * CY)
     v(lambda: V.tensor_copy(T.uoff[:], T.uoi[:]), ["uoi"], ["uoff"], 8)
 
     ts(T.hpw[:], T.l_hp[:], 1.0, None, ALU.add, None, ["l_hp"], ["hpw"], K)
     ts(T.ivw0[:], T.l_iv[:], 1.0, None, ALU.add, None, ["l_iv"], ["ivw0"], K)
-    ts(T.ivs0[:], T.l_iv[:], 1.0 / 512, 1.0 / 512, ALU.mult, ALU.add, ["l_iv"], ["ivs0"], K)
+    ts(fl["ivs0"], T.l_iv[:], 1.0 / 512, 1.0 / 512, ALU.mult, ALU.add, ["l_iv"], ["ivs0"], K)
+    ts(T.udwi[:], T.l_ud[:], 1.0, None, ALU.add, None, ["l_ud"], ["udwi"], K)
+    ts(fl["uds0"], T.l_ud[:], 1.0 / 512, 1.0 / 512, ALU.mult, ALU.add, ["l_ud"], ["uds0"], K)
     ts(T.mtw[:], T.l_mt[:], 1.0, None, ALU.add, None, ["l_mt"], ["mtw"], K)
 
     v(lambda: V.quantize_mx(T.uqc[:, 0:128], T.uqp[:, 0:128], T.ut[:]), ["ut"], ["uq"], 140)
     v(lambda: V.tensor_copy(T.uqsc[:, 0:128].bitcast(U32), T.uqc[:, 0:128].bitcast(U32).indirect(T.uoff[:, 0:8])), ["uq", "uoff"], ["uqsc"], 200)
-    v(lambda: V.tensor_copy(T.uqsp[:, 0:128], T.uqp[:, 0:128].indirect(T.uoff[:, 0:8])), ["uq", "uoff"], ["uqsp"], 200)
+    add(p, ("A",), lambda e: A.activation(T.uqsp[:, 0:128], T.uqp[:, 0:128].indirect(T.uoff[:, 0:8]), ACT.Copy), ["uq", "uoff"], ["uqsp"], 200 * CY)
     for h, (a, b) in enumerate(((0, CUT), (CUT, L))):
         v(lambda a=a, b=b: V.quantize_mx(T.xqc0[:, a:b], T.xqp0[:, a:b], T.x0t[:, 4 * a:4 * b]), ["x0" + "ab"[h]], ["xq0" + "ab"[h]], (b - a) * 1.06 + 14)
     for b in range(4):
@@ -342,49 +373,68 @@ def build(g, core, T, topo):
         add(p, ("N",), None, r, w, 0.0, lat, "n", sem, val)
 
     def ring_ops():
-        v(lambda: V.tensor_copy(win("f0", 0, 449).indirect(T.hpw[:, 0:K]), idc), ["hpw", "idc", "f0i"], ab("f0"), L * 3)
+        gat2(into("f0"), T.ids[:, 512:961], T.hpw, 0, ["hpw", "idc", "idz"], "f0", 0)
+        gat(T.g16[:, 64:80], win("f0", 0, 449), T.o16[:, 8:9], ab("f0") + ["f0i", "o16_s"], ["r16_s"], 32, ("V",))
+        ts(T.o16[:, 0:1], T.g16[:, 64:65], bias[0], None, ALU.add, None, ["r16_s", "bias0"], ["o16_0"], 1)
         for k in range(9):
             fk = win("f%d" % k, 0, 449)
-            if k < 8:
+            if 0 < k < 8:
                 s = relay(win("f%d" % k, 1, 449), T.scr, "scr", ab("f%d" % k))
                 ts(T.fw[:, K * k:K * k + K], s, cp, -512.0, ALU.mult, ALU.add, ["scr", "cp"], ["fw%d" % k], K)
             r0 = ab("f%d" % k) + ["f%di" % k]
             if k < 4:
-                o = T.rrep[:, 0:16] if k == 3 else T.g16[:, 16 * k:16 * k + 16]
+                o = T.rrep[:, L - 16:L] if k == 3 else T.g16[:, 16 * k:16 * k + 16]
                 gat(o, win("f%d" % k, 0, 961), T.o16[:, 2 * k:2 * k + 1], r0 + ["f%dI" % k, "o16_%d" % k], ["r16_%d" % k], 32, ("V",))
                 s = relay(o, T.s16, "s16", ["r16_%d" % k], 16)
                 if k < 3:
                     ts(T.o16[:, 2 * k + 2:2 * k + 3], s, cp, bias[k + 1], ALU.mult, ALU.add, ["s16", "cp", "bias%d" % (k + 1)], ["o16_%d" % (k + 1)], 1)
                 else:
-                    ts(T.rw[:, 0:1], s, cp, -512.0, ALU.mult, ALU.add, ["s16", "cp"], ["rw0"], 1)
+                    ts(T.o16[:, 10:11], s, cp, -512.0, ALU.mult, ALU.add, ["s16", "cp"], ["rwx"], 1)
+                    ts(T.rw[:, K - 1:K], s, cp, -512.0, ALU.mult, ALU.add, ["s16", "cp"], ["rw0"], 1)
             else:
                 b = 1 << (k - 4)
                 n = min(b, K - b)
-                gat(T.rrep[:, 16 * b:16 * b + 16 * n], fk, T.rw[:, 0:n], r0 + ["rw%d" % j for j in range(k - 3)], ["r16_%d" % k], 16 * n)
-                s = relay(T.rrep[:, 16 * b:16 * b + 16 * n], T.s16, "s16", ["r16_%d" % k], 16 * n)
-                ts(T.rw[:, b:b + n], s, cp, -512.0, ALU.mult, ALU.add, ["s16", "cp"], ["rw%d" % (k - 3)], n)
+                e = K - b
+                if n == 1:
+                    gat(T.rrep[:, 16 * (e - n):16 * e], fk, T.o16[:, 10:11], r0 + ["rwx"], ["r16_%d" % k], 16 * n)
+                else:
+                    gat(T.rrep[:, 16 * (e - n):16 * e], fk, T.rw[:, K - n:K], r0 + ["rw%d" % j for j in range(k - 3)], ["r16_%d" % k], 16 * n)
+                s = relay(T.rrep[:, 16 * (e - n):16 * e], T.s16, "s16", ["r16_%d" % k], 16 * n)
+                ts(T.rw[:, e - n:e], s, cp, -512.0, ALU.mult, ALU.add, ["s16", "cp"], ["rw%d" % (k - 3)], n)
             if k < 8:
-                gat2(into("f%d" % (k + 1)), fk, T.fw, K * k, r0 + ["fw%d" % k], "f%d" % (k + 1), CUTS["ring"])
+                gat2(into("f%d" % (k + 1)), fk, T.fw if k else T.hpw, K * k, r0 + (["fw%d" % k] if k else ["hpw"]), "f%d" % (k + 1), CUTS["ring"])
         rws = ["rw%d" % j for j in range(6)]
         v(lambda: V.tensor_copy(T.pmr[:, 0:449].indirect(T.rw[:, 0:K]), T.ids[:, 512:960]), rws + ["idz", "idc"], ["pmr"], L * 3)
         s = relay(T.pmr[:, 1:449], T.scr, "scr", ["pmr"])
         ts(T.pmw[:], s, cp, -512.0, ALU.mult, ALU.add, ["scr", "cp"], ["pmw"], K)
-        ts(T.m1[:], T.rrep[:], 1.0 / 1024, None, ALU.mult, None, ["r16_%d" % k for k in range(3, 9)], ["m1"], L)
+        add(p, ("A",), lambda e: A.activation(T.m1[:], T.rrep[:], ACT.Copy, scale=1.0 / 1024), ["r16_%d" % k for k in range(3, 9)], ["m1"], L * CY)
         tt(T.mono[:], T.m1[:], T.th0[:], ALU.add, ["m1", "th0"], ["mono"], 2 * L)
 
     gat2(into("mtr"), T.ids[:, 512:961], T.mtw, 0, ["mtw", "idc", "idz"], "mtr", 0)
     RW = ["rw%d" % j for j in range(6)]
 
-    def mates_of(m):
-        gat2(lambda a, b: T.mv[:, a:b], win("mtr", 0, 449), T["ivw%d" % m], 0, ab("mtr") + ["mtri", "ivw%d" % m], "mv", 0)
-        s = relay(T.mv[:], T.scm, "scm", ab("mv"))
-        ts(T["mvw%d" % m][:], s, cp, -512.0, ALU.mult, ALU.add, ["scm", "cp"], ["mvw%d" % m], K)
-        ts(T.tiny[:, 0:K], s, cpk, -1.0, ALU.mult, ALU.add, ["scm", "cpk"], ["mvs"], K)
-        tt(T["dm%d" % m][:], T.tiny[:, 0:K], T["ivs%d" % m][:], ALU.subtract, ["mvs", "ivs%d" % m], ["dm%d" % m], 64)
+    def tn(i):
+        return T.tiny[:, K * i:K * i + K]
+
+    gat2(lambda a, b: T.mv[:, a:b], win("mtr", 0, 449), T.ivw0, 0, ab("mtr") + ["mtri", "ivw0"], "mv", 0)
+    s = relay(T.mv[:], T.scm, "scm", ab("mv"))
+    ts(T.mvw0[:], s, cp, -512.0, ALU.mult, ALU.add, ["scm", "cp"], ["mvw0"], K)
+    ts(tn(0), s, cpk, -1.0, ALU.mult, ALU.add, ["scm", "cpk"], ["mvs0"], K)
+    tt(fl["dm0"], tn(0), fl["ivs0"], ALU.subtract, ["mvs0", "ivs0"], ["dm0"], 64)
+    tt(tn(1), tn(0), T.jws[:], ALU.is_gt, ["mvs0", "jws"], ["zm0"], 64)
+    tt(tn(2), tn(0), tn(1), ALU.add, ["mvs0", "zm0"], ["zm1"], 64)
+    tt(tn(3), fl["ivs0"], T.jws[:], ALU.is_gt, ["ivs0", "jws"], ["zi0"], 64)
+    tt(fl["z0"], fl["ivs0"], tn(3), ALU.add, ["ivs0", "zi0"], ["z0"], 64)
+    tt(fl["dz0"], tn(2), fl["z0"], ALU.subtract, ["zm1", "z0"], ["dz0"], 64)
+    gat2(into("udrep"), T.ids[:, 512:961], T.udwi, 0, ["udwi", "idc", "idz"], "udrep", 0)
+    gat2(lambda a, b: T.um[:, a:b], win("udrep", 0, 449), T.mtw, 0, ab("udrep") + ["udrepi", "mtw"], "um", 0)
+    s = relay(T.um[:], T.scu, "scu", ab("um"))
+    ts(tn(4), s, cpk, -1.0, ALU.mult, ALU.add, ["scu", "cpk"], ["mus"], K)
+    tt(fl["dmu0"], tn(4), fl["uds0"], ALU.subtract, ["mus", "uds0"], ["dmu0"], 64)
 
     def places(sc, sck, out, key, i):
         t = T.ti
-        ts(t[:, 2 * K * i:2 * K * i + K], sc[:, 15:L:16], cp, 1024.0, ALU.mult, ALU.mult, [sck, "cp"], ["ti%da" % i], K)
+        ts(t[:, 2 * K * i:2 * K * i + K], sc[:, 15:L:16], cp, 1024.0, ALU.mult, ALU.mult, sck + ["cp"], ["ti%da" % i], K)
         ts(t[:, 2 * K * i + K:2 * K * i + 2 * K], t[:, 2 * K * i:2 * K * i + K], 511, None, ALU.bitwise_and, None, ["ti%da" % i], ["ti%db" % i], K)
         v(lambda: V.tensor_copy(out[:], t[:, 2 * K * i + K:2 * K * i + 2 * K]), ["ti%db" % i], [key], K)
 
@@ -406,7 +456,6 @@ def build(g, core, T, topo):
             return V.tensor_copy(out, t[:, o:o + n]) if scale == 1.0 else V.tensor_scalar(out, t[:, o:o + n], scale, None, ALU.mult)
         add(p, ("V", "A"), fn, [], ["bank%d" % i] + w, 0.02 + n * CY)
 
-    mates_of(0)
     for m in range(NR):
         dst = T.cores[rank ^ STEP[m]]
         n8 = len(topo.engines(core, dst))
@@ -416,23 +465,43 @@ def build(g, core, T, topo):
         send(dst, lc[:].bitcast(U8), xc[:].bitcast(U8), "rc%d" % m, X, [], 0, "out_c%d" % m)
         send(dst, lp[:], xp[:], "rc%d" % m, X, [], 0, "out_s%d" % m)
         arrive("rc%d" % m, 2 * n8, ["out_c%d" % m, "out_s%d" % m], ["la%d" % m], 6.0)
-        mm(4, T.uqsc, T.uqsp, 0, xc, xp, 0, L, X + ["uqsc", "uqsp"])
-        ts(T.sgn[:, 1:449], T.pb[:, 0:L], 0.0, 1.0, ALU.is_gt, ALU.add, [], ["bank4", "sgn"], L)
-        gat(T.ga[:], T.sgn[:, 0:449], T["ivw%d" % m][:, 0:K], ["sgn", "sgni", "ivw%d" % m], ["ga"], L, ("V",))
-        gat(T.gb[:], T.sgn[:, 0:449], T["mvw%d" % m][:, 0:K], ["sgn", "sgni", "mvw%d" % m], ["gb"], L, ("A",))
+        for h in (0, 1):
+            mm(4 + h, T.uqsc, T.uqsp, 0, xc, xp, 224 * h, 224 * h + 224, X + ["uqsc", "uqsp"])
+            ts(T.sgn[:, 1 + 224 * h:225 + 224 * h], T.pb[:, 512 * h:512 * h + 224], 0.0, 1.0, ALU.is_gt, ALU.add, [], ["bank%d" % (4 + h), "sgn%d" % h], 224)
+        SG = ["sgn0", "sgn1"]
+        gat(T.ga[:], T.sgn[:, 0:449], T["ivw%d" % m][:, 0:K], SG + ["sgni", "ivw%d" % m], ["ga"], L, ("V",))
+        gat(T.gb[:], T.sgn[:, 0:449], T["mvw%d" % m][:, 0:K], SG + ["sgni", "mvw%d" % m], ["gb"], L, ("A",))
         for a in "ab":
             v(lambda a=a: V.tensor_tensor_scan(T["y" + a][:], T.db[:], T["g" + a][:], 0.0, ALU.mult, ALU.max), ["db", "g" + a], ["y" + a], L // 2)
-        tn = [T.tiny[:, K * i:K * i + K] for i in range(12)]
-        tt(tn[1], T.ya[:, 15:L:16], T.yb[:, 15:L:16], ALU.mult, ["ya", "yb"], ["t1"], 64)
-        ts(tn[2], tn[1], thr, None, ALU.is_ge, None, ["t1", "thr"], ["t2"], K)
-        tt(tn[3], tn[2], T["dm%d" % m][:], ALU.mult, ["t2", "dm%d" % m], ["t3"], 64)
-        tt(T["ivs%d" % nx][:], tn[3], T["ivs%d" % m][:], ALU.add, ["t3", "ivs%d" % m], ["ivs%d" % nx], 64)
-        tt(tn[4], T["ivs%d" % nx][:], T.jws[:], ALU.is_gt, ["ivs%d" % nx, "jws"], ["t4"], 64)
-        tt(tn[5], tn[4], T["ivs%d" % nx][:], ALU.add, ["t4", "ivs%d" % nx], ["t5"], 64)
+        t1, t2, t3, t6, t7 = [tn(i) for i in (5, 6, 7, 8, 9)]
+        tt(t1, T.ya[:, 15:L:16], T.yb[:, 15:L:16], ALU.mult, ["ya", "yb"], ["t1"], 64)
+        ts(t2, t1, thr, None, ALU.is_ge, None, ["t1", "thr"], ["t2"], K)
+        tt(t3, t2, fl["dz%d" % m], ALU.mult, ["t2", "dz%d" % m], ["t3"], 64)
+        tt(fl["z%d" % nx], t3, fl["z%d" % m], ALU.add, ["t3", "z%d" % m], ["z%d" % nx], 64)
         zo = T["zo%d" % m]
-        ts(zo[:], tn[5], 512.0, None, ALU.mult, None, ["t5"], ["zo%d" % m], K)
+        ts(zo[:], fl["z%d" % nx], 512.0, None, ALU.mult, None, ["z%d" % nx], ["zo%d" % m], K)
+        tt(t6, t2, fl["dm%d" % m], ALU.mult, ["t2", "dm%d" % m], ["t6"], 64)
+        tt(fl["ivs%d" % nx], t6, fl["ivs%d" % m], ALU.add, ["t6", "ivs%d" % m], ["ivs%d" % nx], 64)
         ivw = T["ivw%d" % nx]
-        ts(ivw[:], T["ivs%d" % nx][:], 512.0, None, ALU.mult, None, ["ivs%d" % nx], ["ivw%d" % nx], K)
+        if nx < NR:
+            ts(t7, t2, -2.0, 1.0, ALU.mult, ALU.add, ["t2"], ["t7"], K)
+            for n in ("dm", "dz"):
+                tt(fl["%s%d" % (n, nx)], t7, fl["%s%d" % (n, m)], ALU.mult, ["t7", "%s%d" % (n, m)], ["%s%d" % (n, nx)], 64)
+            tt(tn(10), fl["ivs%d" % nx], fl["dm%d" % nx], ALU.add, ["ivs%d" % nx, "dm%d" % nx], ["mvs"], 64)
+            ts(T["mvw%d" % nx][:], tn(10), 512.0, None, ALU.mult, None, ["mvs"], ["mvw%d" % nx], K)
+        gat(T.gm[:], T.sgn[:, 0:449], T.mtw[:, 0:K], SG + ["sgni", "mtw"], ["gm"], L, ("A",))
+        v(lambda: V.tensor_tensor_scan(T.yc[:], T.db[:], T.sgn[:, 1:449], 0.0, ALU.mult, ALU.max), ["db"] + SG, ["yc"], L // 2)
+        v(lambda: V.tensor_tensor_scan(T.yd[:], T.db[:], T.gm[:], 0.0, ALU.mult, ALU.max), ["db", "gm"], ["yd"], L // 2)
+        u1, u2, u3, u4 = [tn(i) for i in (11, 12, 13, 14)]
+        tt(u1, T.yc[:, 15:L:16], T.yd[:, 15:L:16], ALU.mult, ["yc", "yd"], ["u1"], 64)
+        ts(u2, u1, thr, None, ALU.is_ge, None, ["u1", "thr"], ["u2"], K)
+        tt(u3, u2, fl["dmu%d" % m], ALU.mult, ["u2", "dmu%d" % m], ["u3"], 64)
+        tt(fl["uds%d" % nx], u3, fl["uds%d" % m], ALU.add, ["u3", "uds%d" % m], ["uds%d" % nx], 64)
+        ts(T["udw%d" % m][:], fl["uds%d" % nx], 512.0, None, ALU.mult, None, ["uds%d" % nx], ["udw%d" % m], K)
+        if nx < NR:
+            ts(u4, u2, -2.0, 1.0, ALU.mult, ALU.add, ["u2"], ["u4"], K)
+            tt(fl["dmu%d" % nx], u4, fl["dmu%d" % m], ALU.mult, ["u4", "dmu%d" % m], ["dmu%d" % nx], 64)
+        ts(ivw[:], fl["ivs%d" % nx], 512.0, None, ALU.mult, None, ["ivs%d" % nx], ["ivw%d" % nx], K)
         send(dst, T["liv%d" % m][:], ivw[:], "ri%d" % m, ["ivw%d" % nx], [], 0, "out_i%d" % m)
         arrive("ri%d" % m, n8, ["out_i%d" % m], ["liv%d" % m], 2.0)
         first = min(m, 1)
@@ -442,8 +511,8 @@ def build(g, core, T, topo):
         for lv in range(LV):
             A_, B_, C_ = ["p%d" % i for i in (a, b, c)]
             o = K * lv
-            s = relay(win(A_, 1, 449), T.sc, "sc", ab(A_))
-            ts(T.offw[:, o:o + K], s, cp, -512.0, ALU.mult, ALU.add, ["sc", "cp"], ["offw%d" % lv], K)
+            s, sk = relay2(A_, "sc", CUTS["c" if lv else "w"][first] if SPLIT else 0)
+            ts(T.offw[:, o:o + K], s, cp, -512.0, ALU.mult, ALU.add, sk + ["cp"], ["offw%d" % lv], K)
             gat2(into(B_), win(A_, 0, 450), T.offw, o, ab(A_) + [A_ + "i", A_ + "j", "offw%d" % lv], B_, CUTS["b"][first])
             gat2(into(C_), win(B_, 0, 450), T.offw, o, ab(B_) + [B_ + "i", B_ + "j", "offw%d" % lv], C_, CUTS["c"][first])
             a, c = c, a
@@ -453,13 +522,13 @@ def build(g, core, T, topo):
         gat2(lambda a, b: T.vr[:, a:b], win(A_, 0, 450), T.rw, 0, ab(A_) + [A_ + "i", A_ + "j"] + RW, "vr", CUTS["r"])
         v(lambda: V.tensor_tensor_scan(win("st", 1, 449), T.vr[:], T.mono[:], 512.0, ALU.max, ALU.min), ab("vr") + ["mono"], ["st"], L)
         gat2(into("bwin"), win("st", 0, 449), T.pmw, 0, ["st", "sti", "pmw"], "bwin", CUTS["r"])
-        relay(win("bwin", 1, 449), T.sc, "sc", ab("bwin"))
-        places(T.sc, "sc", T["bw%d" % m], "bw%d" % m, 0)
+        s, sk = relay2("bwin", "sc", CUTS["r"] if SPLIT else 0)
+        places(T.sc, sk, T["bw%d" % m], "bw%d" % m, 0)
         send(dst, T["lbw%d" % m][:], T["bw%d" % m][:], "rb%d" % m, ["bw%d" % m], [], 0, "out_b%d" % m)
         arrive("rb%d" % m, n8, ["out_b%d" % m], ["lbw%d" % m], 2.0)
         gat2(lambda a, b: T.eb[:, a:b], win("bwin", 0, 449), T["liv%d" % m], 0, ab("bwin") + ["bwini", "liv%d" % m], "eb", 0)
         relay(T.eb[:], T.scb, "scb", ab("eb"))
-        places(T.scb, "scb", T["ew%d" % m], "ew%d" % m, 1)
+        places(T.scb, ["scb"], T["ew%d" % m], "ew%d" % m, 1)
         send(dst, T["lew%d" % m][:], T["ew%d" % m][:], "re_%d" % m, ["ew%d" % m], [], 0, "out_e%d" % m)
         arrive("re_%d" % m, n8, ["out_e%d" % m], ["lew%d" % m], 2.0)
         for b in range(4):
@@ -469,10 +538,7 @@ def build(g, core, T, topo):
             mm(4 + b, T.eqc, T.eqp, 128 * b, lc, lp, 0, L, ["la%d" % m, "eq%d" % b])
             unload(4 + b, T.tp[:, TW * b + 1:TW * b + 449], L, 1.0, ["tp%d" % b])
         for b in range(4):
-            gat(T.g1[:, L * b:L * b + L], T.tp[:, TW * b:TW * b + 449], T["liv%d" % m][:, 0:K], ["tp%d" % b, "tpi%d" % b, "liv%d" % m], ["g1%d" % b], L)
-        v(lambda ivw=ivw: V.tensor_copy(T.udr[:, 0:449].indirect(ivw[:, 0:K]), idc), ["ivw%d" % nx, "idc"], ["udr"], L * 3)
-        s = relay(T.udr[:, 1:449], T.scu, "scu", ["udr"])
-        ts(T["udw%d" % m][:], s, cp, -512.0, ALU.mult, ALU.add, ["scu", "cp"], ["udw%d" % m], K)
+            gat(T.g1[:, L * b:L * b + L], T.tp[:, TW * b:TW * b + 449], T["liv%d" % m][:, 0:K], ["tp%d" % b, "tpi%d" % b, "liv%d" % m], ["g1%d" % b], L, G1)
         for b in range(4):
             gat(T.g2[:, L * b:L * b + L], T.to[:, TW * b:TW * b + 449], T["udw%d" % m][:, 0:K], ["to%d" % b, "toi%d" % b, "udw%d" % m], ["g2%d" % b], L)
         for h, (c0, c1) in enumerate(((0, CUT), (CUT, L))):
@@ -489,8 +555,6 @@ def build(g, core, T, topo):
             v(lambda b=b, m=m: V.tensor_tensor(T.xnt[:, b:4 * L:4], T.hh[:, TW * b:TW * b + 449].indirect(T["lew%d" % m][:, 0:K]), T.g2[:, L * b:L * b + L], ALU.add),
               ["hh%d0" % b, "hh%d1" % b, "hhi%d" % b, "lew%d" % m, "g2%d" % b], ["xnt%d" % b], 60 + L * GC)
         v(lambda nx=nx: V.quantize_mx(T["xqc%d" % nx][:], T["xqp%d" % nx][:], T.xnt[:]), ["xnt%d" % b for b in range(4)], ["xq%da" % nx, "xq%db" % nx], 14 + L * 1.06)
-        if nx < NR:
-            mates_of(nx)
 
     outs = [0]
 
@@ -498,7 +562,8 @@ def build(g, core, T, topo):
         outs[0] += 16
         add(p, (q,), lambda e: (g.sync if e == "S" else g.scalar).dma_start(out, in_), r, ["st%d" % outs[0]], 0.05, 2.0, "d", "d_out")
     X = ["xq3a", "xq3b"]
-    ts(T.uf[:], T.udr[:, 1:449], -513.0, None, ALU.add, None, ["udr"], ["uf"], L)
+    gat2(lambda a, b: T.uf0[:, a:b], T.ids[:, 512:961], T["udw%d" % (NR - 1)], 0, ["udw%d" % (NR - 1), "idc", "idz"], "uf0", 0)
+    ts(T.uf[:], T.uf0[:], -513.0, None, ALU.add, None, ab("uf0"), ["uf"], L)
     store("S", T.uo[:], T.uf[0:128:16, :], ["uf"])
     v(lambda: V.quantize_mx(T.vqc[:], T.vqp[:], T.vt[:]), ["vt"], ["vq"], 140)
     mm(4, T.vqc, T.vqp, 0, T.xqc3, T.xqp3, 0, L, X + ["vq"])

@@ -9,6 +9,7 @@ NR = 3
 STEP = [1, 2, 3]
 CUT = 256
 CUTS = {"ring": 0, "w": (0, 12), "b": (0, 14), "c": (0, 12), "r": 12}
+PARTS = ((0, CUT), (CUT, L))
 LV = 5
 TW = 464
 
@@ -76,6 +77,8 @@ _buf("ti", 4 * K, "int32")
 _buf("pcol", 8, "int32")
 _buf("col", 16)
 _buf("ones", 16)
+_buf("half", 16)
+_buf("cps", 16)
 _buf("to", 4 * TW, "bfloat16")
 _buf("tp", 4 * TW, "bfloat16")
 _buf("hh", 4 * TW, "bfloat16")
@@ -88,19 +91,19 @@ LOADS = ["d_hp", "d_iv", "d_mt", "d_ud", "d_u", "d_xa", "d_xb", "d_v", "d_wc", "
 SEMAPHORES = ["sv", "sa", "sp", "sg", "sent", "d_out"] + LOADS + ["%s%d" % (a, m) for a in ("rc", "ri", "rb", "re_") for m in range(NR)]
 SEM = {"V": "sv", "A": "sa", "P": "sp", "G": "sg"}
 CY = 0.00083
-GC = 1.5
-WAKE = 0.08
 DELTA = 0.12
 AHEAD = 0.8
-G1 = ("A",)
+G1 = ("V", "A")
 SPLIT = True
+KTOP = 6
+BOOST = (30.0, 0.0)
 
 
 def new_prog():
-    return {"ops": [], "wr": {}, "rd": {}}
+    return {"ops": [], "wr": {}, "rd": {}, "boost": 0.0, "tag": ""}
 
 
-def add(p, eng, fn, r, w, dur, lat=0.0, kind="c", sem=None, val=1):
+def add(p, eng, fn, r, w, dur, lat=0.0, kind="c", sem=None, val=1, ge=0):
     ops = p["ops"]
     i = len(ops)
     deps = set()
@@ -120,66 +123,158 @@ def add(p, eng, fn, r, w, dur, lat=0.0, kind="c", sem=None, val=1):
         p["wr"][k] = i
         p["rd"][k] = []
     deps.discard(i)
-    ops.append({"eng": eng, "fn": fn, "deps": sorted(deps), "dur": dur, "lat": lat, "kind": kind, "sem": sem, "val": val})
+    ops.append({"boost": p["boost"], "tag": p["tag"], "eng": eng, "fn": fn, "deps": sorted(deps), "dur": dur, "ge": ge, "lat": lat, "kind": kind, "sem": sem, "val": val})
     return i
 
 
-TRIES = 24
-NOISE = 0.6
+MOVES = 16000
+COSTS = [(1.5, 1.2, 0.08, 1.0), (1.1, 1.1, 0.05, 1.4), (2.0, 1.3, 0.12, 0.8)]
+LIFT = {"iv": 8.0, "tp": 3.0, "ga": 3.0, "ud": 3.0}
+FOUND = {}
 
 
 def order(ops):
-    best = None
-    for k in range(TRIES):
-        s = schedule(ops, k)
-        if best is None or s[2] < best[2]:
-            best = s
-    return best
+    key = (len(ops), sum(len(o["deps"]) for o in ops))
+    if key not in FOUND:
+        FOUND[key] = better(ops, *schedule(ops))
+    return FOUND[key]
 
 
-def schedule(ops, seed):
+def cost(o, c):
+    return (o["dur"] + o["ge"] * c[0] * CY) * c[1]
+
+
+def walk(ops, seq, on, c, durs, paths):
+    free, end, before, why = {}, [0.0] * len(ops), {}, {}
+    wake, late = c[2], c[3]
+    for i in seq:
+        o = ops[i]
+        t, b = 0.0, None
+        for d in o["deps"]:
+            x = end[d] + wake
+            if x > t:
+                t, b = x, (d, False)
+        e, k = on[i], durs[i]
+        if e != "N":
+            f = free.get(e, 0.0)
+            if f > t:
+                t, b = f, (before[e], True)
+            free[e] = t + k
+            before[e] = i
+        end[i] = t + k + o["lat"] * late
+        if paths:
+            why[i] = b
+    if not paths:
+        return max(end)
+    i = max(seq, key=lambda i: end[i])
+    found = []
+    while why[i] is not None:
+        if why[i][1]:
+            found.append((i, why[i][0]))
+        i = why[i][0]
+    return found
+
+
+def better(ops, seq, on):
     n = len(ops)
-    rng = np.random.RandomState(seed)
+    rng = np.random.RandomState(3)
+    succ = [[] for _ in range(n)]
+    for i, o in enumerate(ops):
+        for d in o["deps"]:
+            succ[d].append(i)
+    durs = [[cost(o, c) for o in ops] for c in COSTS]
+
+    def total(s, o):
+        return sum(walk(ops, s, o, c, k, False) for c, k in zip(COSTS, durs))
+    now = total(seq, on)
+    best, path = (now, seq, on), None
+    dice = rng.random_sample((MOVES, 6)).tolist()
+    for k in range(MOVES):
+        r = dice[k]
+        if path is None or k % 15 == 0:
+            c = int(r[5] * len(COSTS))
+            path = walk(ops, seq, on, COSTS[c], durs[c], True)
+        if not path:
+            continue
+        i, j = path[int(r[0] * len(path))]
+        seq2, on2 = seq, on
+        flex = [x for x in (i, j) if len(ops[x]["eng"]) > 1]
+        if r[1] < 0.15 and flex:
+            x = flex[int(r[2] * len(flex))]
+            on2 = list(on)
+            on2[x] = "A" if on[x] == "V" else "V"
+        else:
+            pi, pj = seq.index(i), seq.index(j)
+            if pi < pj:
+                continue
+            far = int(r[3] * 60) if r[4] < 0.4 else 0
+            if r[1] < 0.6:
+                needs = set(succ[j])
+                to = pi + 1
+                if any(x in needs for x in seq[pj + 1:to]):
+                    continue
+                while far and to < n and seq[to] not in needs:
+                    to, far = to + 1, far - 1
+                seq2 = seq[:pj] + seq[pj + 1:to] + [j] + seq[to:]
+            else:
+                needs = set(ops[i]["deps"])
+                to = pj
+                if any(x in needs for x in seq[to:pi]):
+                    continue
+                while far and to > 0 and seq[to - 1] not in needs:
+                    to, far = to - 1, far - 1
+                seq2 = seq[:to] + [i] + seq[to:pi] + seq[pi + 1:]
+        t = total(seq2, on2)
+        if t <= now + 0.25 * (1 - k / MOVES) * r[2] ** 2:
+            if t != now:
+                path = None
+            seq, on, now = seq2, on2, t
+            if t < best[0] - 1e-9:
+                best = (t, seq, on)
+    return best[1], best[2]
+
+
+def schedule(ops):
+    n = len(ops)
+    WAKE = COSTS[0][2]
+    dur = [cost(o, COSTS[0]) for o in ops]
     succ = [[] for _ in range(n)]
     for i, o in enumerate(ops):
         for d in o["deps"]:
             succ[d].append(i)
     prio = [0.0] * n
     for i in range(n - 1, -1, -1):
-        o = ops[i]
-        prio[i] = o["dur"] + o["lat"] + WAKE + max([prio[s] for s in succ[i]] + [0.0])
-    if seed:
-        prio = [a + NOISE * float(b) for a, b in zip(prio, rng.standard_normal(n))]
+        prio[i] = dur[i] + ops[i]["lat"] + WAKE + max([prio[s] for s in succ[i]] + [0.0])
     free, left = {}, [len(o["deps"]) for o in ops]
     end, when, on = [0.0] * n, [0.0] * n, [None] * n
-    ready = [i for i in range(n) if not left[i]]
+    ready = {i: 0.0 for i in range(n) if not left[i]}
     while ready:
         cand = []
-        for i in ready:
-            at = max([end[d] + WAKE for d in ops[i]["deps"]] + [0.0])
+        for i, at in ready.items():
             for e in ops[i]["eng"]:
-                cand.append((max(at, free.get(e, 0.0)) if e != "N" else at, i, e))
-        t0 = min(c[0] for c in cand)
-        first = min(c for c in cand if c[0] == t0)
-        eng = [c for c in cand if c[2] == first[2] and c[0] <= t0 + max(DELTA, AHEAD * ops[first[1]]["dur"])]
-        t, i, e = max(eng, key=lambda c: (prio[c[1]] - (c[0] - t0), -c[1]))
+                f = free.get(e, 0.0)
+                cand.append((at if at > f else f, i, e))
+        first = min(cand)
+        t0 = first[0]
+        late = t0 + max(DELTA, AHEAD * dur[first[1]])
+        t, i, e = max([c for c in cand if c[2] == first[2] and c[0] <= late], key=lambda c: (prio[c[1]] - (c[0] - t0), -c[1]))
         o = ops[i]
-        ready.remove(i)
+        del ready[i]
         when[i], on[i] = t, e
         if e != "N":
-            free[e] = t + o["dur"]
-        end[i] = t + o["dur"] + o["lat"]
+            free[e] = t + dur[i]
+        end[i] = t + dur[i] + o["lat"]
         for s in succ[i]:
             left[s] -= 1
             if not left[s]:
-                ready.append(s)
-    seq = sorted(range(n), key=lambda i: (when[i], i))
-    return seq, on, max(end), when, end
+                ready[s] = max(end[d] + WAKE for d in ops[s]["deps"])
+    return sorted(range(n), key=lambda i: (when[i], i)), on
 
 
 def emit(g, T, p):
     ops = p["ops"]
-    seq, on, total, when, end = order(ops)
+    seq, on = order(ops)
+    when = {i: k for k, i in enumerate(seq)}
     q = {"V": g.vector, "A": g.scalar, "P": g.tensor, "G": g, "S": g.sync}
     count = {e: 0 for e in q}
     known = {e: {} for e in q}
@@ -217,7 +312,7 @@ def emit(g, T, p):
             c[o["sem"]] = 16
         clock[i] = c
         ops[i]["n"] = count[e]
-    return count, known, total
+    return count
 
 
 def own(ops, on, clock, d):
@@ -233,8 +328,8 @@ def build(g, core, T, topo):
     V, A, P, G = g.vector, g.scalar, g.tensor, g
     U8, U32 = dt.uint8, dt.uint32
 
-    def v(fn, r, w, el):
-        return add(p, ("V",), lambda e: fn(), r, w, max(64, el) * CY)
+    def v(fn, r, w, el, ge=0):
+        return add(p, ("V",), lambda e: fn(), r, w, (el if ge else max(64, el)) * CY, ge=ge)
 
     def ts(out, in0, s1, s2, op0, op1, r, w, el):
         if op1 is None:
@@ -252,7 +347,7 @@ def build(g, core, T, topo):
             if e == "V":
                 return V.tensor_copy(out, win.indirect(off))
             return A.activation(out, win.indirect(off), ACT.Copy)
-        return add(p, eng, fn, r, w, 0.055 + el * GC * CY)
+        return add(p, eng, fn, r, w, 0.055, ge=el)
 
     def win(n, a, b):
         t, o = WIN[n]
@@ -260,9 +355,8 @@ def build(g, core, T, topo):
 
     def gat2(out, window, off, oo, r, key, cut):
         h = 16 * cut
-        o = out if cut in (0, K) else None
-        if cut in (0, K):
-            gat(out(0, L), window, off[:, oo:oo + K], r, [key + "a", key + "b"], L, ("A",) if cut == 0 else ("V",))
+        if cut in (-1, 0, K):
+            gat(out(0, L), window, off[:, oo:oo + K], r, [key + "a", key + "b"], L, ("V", "A") if cut < 0 else ("A",) if cut == 0 else ("V",))
             return
         gat(out(0, h), window, off[:, oo:oo + cut], r, [key + "a"], h, ("V",))
         gat(out(h, L), window, off[:, oo + cut:oo + K], r, [key + "b"], L - h, ("A",))
@@ -279,13 +373,14 @@ def build(g, core, T, topo):
 
     def relay2(key, sck, cut):
         h = 16 * cut
-        if cut in (0, K):
+        if cut in (-1, 0, K):
             return relay(win(key, 1, 1 + L), T.sc, sck + "b", ab(key)), [sck + "b"]
         for a, b, c in ((0, h, "a"), (h, L, "b")):
             v(lambda a=a, b=b: V.tensor_tensor_scan(T.sc[:, a:b], T.d2[:, a:b], win(key, 1 + a, 1 + b), 0.0, ALU.mult, ALU.max), [key + c, "d2"], [sck + c], b - a)
         return T.sc[:, 15:L:16], ab(sck)
 
-    cp, cpk, pw, thr, kf = [T.col[:, i:i + 1] for i in (0, 1, 2, 3, 4)]
+    cp = T.cps[:, 15:16]
+    cpk, kf = T.col[:, 1:2], T.col[:, 4:5]
     bias = [T.col[:, 8 + k:9 + k] for k in range(4)]
     idc = T.ids[:, 513:961]
     fl = {n: T.lst[:, K * i:K * i + K] for i, n in enumerate(FLOATS)}
@@ -322,12 +417,9 @@ def build(g, core, T, topo):
     ts(T.pcol[:, 1:2], T.pcol[:, 0:1], 15, None, ALU.bitwise_and, None, ["pcol"], ["kint"], 1)
     v(lambda: V.tensor_copy(kf, T.pcol[:, 1:2]), ["kint"], ["kf"], 1)
     ts(T.d2[:], T.tmod[:], kf, 2.0, ALU.is_gt, ALU.mult, ["tmod", "kf"], ["d2"], L)
-    relay(T.ones[:], T.s16, "s16", ["ones"], 16)
-    v(lambda: V.tensor_copy(pw, T.s16[:, 15:16]), ["s16"], ["pw"], 1)
-    v(lambda: V.reciprocal(cp, pw), ["pw"], ["cp"], 300)
+    ts(T.half[:], T.d2[:, 0:16], -0.25, 1.0, ALU.mult, ALU.add, ["d2"], ["half"], 16)
+    v(lambda: V.tensor_tensor_scan(T.cps[:], T.half[:], T.ones[:], 1.0, ALU.mult, ALU.min), ["half", "ones"], ["cp"], 16)
     ts(cpk, cp, 1.0 / 512, None, ALU.mult, None, ["cp"], ["cpk"], 1)
-    tt(T.col[:, 5:6], pw, pw, ALU.mult, ["pw"], ["pw2"], 1)
-    ts(thr, T.col[:, 5:6], 4.0, None, ALU.mult, None, ["pw2"], ["thr"], 1)
     for k in range(4):
         ts(T.pcol[:, 2 + k:3 + k], T.pcol[:, 0:1], 1 << k, None, ALU.bitwise_and, None, ["pcol"], ["bit%d" % k], 1)
         ts(bias[k], T.pcol[:, 2 + k:3 + k], 512.0 / (1 << k), -512.0, ALU.mult, ALU.add, ["bit%d" % k], ["bias%d" % k], 1)
@@ -347,7 +439,9 @@ def build(g, core, T, topo):
         A.activation(T.th0[:], idc, ACT.Copy, bias=255.0, scale=0.5), ["idc"], ["th0"], L * CY)
     v(lambda: V.tensor_copy(T.uoff[:], T.uoi[:]), ["uoi"], ["uoff"], 8)
 
+    p["boost"] = BOOST[0]
     ts(T.hpw[:], T.l_hp[:], 1.0, None, ALU.add, None, ["l_hp"], ["hpw"], K)
+    p["boost"] = 0.0
     ts(T.ivw0[:], T.l_iv[:], 1.0, None, ALU.add, None, ["l_iv"], ["ivw0"], K)
     ts(fl["ivs0"], T.l_iv[:], 1.0 / 512, 1.0 / 512, ALU.mult, ALU.add, ["l_iv"], ["ivs0"], K)
     ts(T.udwi[:], T.l_ud[:], 1.0, None, ALU.add, None, ["l_ud"], ["udwi"], K)
@@ -372,13 +466,25 @@ def build(g, core, T, topo):
     def arrive(sem, val, r, w, lat):
         add(p, ("N",), None, r, w, 0.0, lat, "n", sem, val)
 
+    RW, MONO = [], []
+
     def ring_ops():
+        p["boost"] = BOOST[1]
         gat2(into("f0"), T.ids[:, 512:961], T.hpw, 0, ["hpw", "idc", "idz"], "f0", 0)
         gat(T.g16[:, 64:80], win("f0", 0, 449), T.o16[:, 8:9], ab("f0") + ["f0i", "o16_s"], ["r16_s"], 32, ("V",))
         ts(T.o16[:, 0:1], T.g16[:, 64:65], bias[0], None, ALU.add, None, ["r16_s", "bias0"], ["o16_0"], 1)
-        for k in range(9):
+
+        def piece(lo, hi, r):
+            a, b = 16 * lo, 16 * hi
+            v(lambda: V.tensor_copy(T.pmr[:, 0:449].indirect(T.rw[:, lo:hi]), T.ids[:, 512 + a:512 + b]), r + ["idz", "idc"], ["pmr"], 60 + (b - a) * 3)
+            add(p, ("V", "A"), lambda e: A.activation(T.m1[:, a:b], T.rrep[:, a:b], ACT.Copy, scale=1.0 / 1024) if e == "A" else
+                V.tensor_scalar(T.m1[:, a:b], T.rrep[:, a:b], 1.0 / 1024, None, ALU.mult), r, ["m1_%d" % lo], max(64, b - a) * CY)
+            tt(T.mono[:, a:b], T.m1[:, a:b], T.th0[:, a:b], ALU.add, ["m1_%d" % lo, "th0"], ["mono%d" % lo], 2 * (b - a))
+            MONO.append("mono%d" % lo)
+
+        for k in range(KTOP + 1):
             fk = win("f%d" % k, 0, 449)
-            if 0 < k < 8:
+            if 0 < k < KTOP:
                 s = relay(win("f%d" % k, 1, 449), T.scr, "scr", ab("f%d" % k))
                 ts(T.fw[:, K * k:K * k + K], s, cp, -512.0, ALU.mult, ALU.add, ["scr", "cp"], ["fw%d" % k], K)
             r0 = ab("f%d" % k) + ["f%di" % k]
@@ -390,28 +496,32 @@ def build(g, core, T, topo):
                     ts(T.o16[:, 2 * k + 2:2 * k + 3], s, cp, bias[k + 1], ALU.mult, ALU.add, ["s16", "cp", "bias%d" % (k + 1)], ["o16_%d" % (k + 1)], 1)
                 else:
                     ts(T.o16[:, 10:11], s, cp, -512.0, ALU.mult, ALU.add, ["s16", "cp"], ["rwx"], 1)
-                    ts(T.rw[:, K - 1:K], s, cp, -512.0, ALU.mult, ALU.add, ["s16", "cp"], ["rw0"], 1)
+                    ts(T.rw[:, K - 1:K], s, cp, -512.0, ALU.mult, ALU.add, ["s16", "cp"], ["rw%d" % (K - 1)], 1)
+                    RW.append("rw%d" % (K - 1))
             else:
                 b = 1 << (k - 4)
-                n = min(b, K - b)
-                e = K - b
-                if n == 1:
-                    gat(T.rrep[:, 16 * (e - n):16 * e], fk, T.o16[:, 10:11], r0 + ["rwx"], ["r16_%d" % k], 16 * n)
-                else:
-                    gat(T.rrep[:, 16 * (e - n):16 * e], fk, T.rw[:, K - n:K], r0 + ["rw%d" % j for j in range(k - 3)], ["r16_%d" % k], 16 * n)
-                s = relay(T.rrep[:, 16 * (e - n):16 * e], T.s16, "s16", ["r16_%d" % k], 16 * n)
-                ts(T.rw[:, e - n:e], s, cp, -512.0, ALU.mult, ALU.add, ["s16", "cp"], ["rw%d" % (k - 3)], n)
-            if k < 8:
+                c = b
+                while c < K and (c == b or k == KTOP):
+                    c1 = min(c + b, K)
+                    lo, hi = K - c1, K - c
+                    blk = 16 * (hi - lo)
+                    if b == 1:
+                        gat(T.rrep[:, 16 * lo:16 * hi], fk, T.o16[:, 10:11], r0 + ["rwx"], ["rr%d" % lo], 16, ("V",))
+                    else:
+                        gat(T.rrep[:, 16 * lo:16 * hi], fk, T.rw[:, lo + b:hi + b], r0 + [x for x in RW if lo + b <= int(x[2:]) < hi + b], ["rr%d" % lo], blk)
+                    s = relay(T.rrep[:, 16 * lo:16 * hi], T.s16, "s16", ["rr%d" % lo], blk)
+                    ts(T.rw[:, lo:hi], s, cp, -512.0, ALU.mult, ALU.add, ["s16", "cp"], ["rw%d" % lo], hi - lo)
+                    RW.append("rw%d" % lo)
+                    piece(lo, hi if b > 1 else K, ["rw%d" % lo, "rr%d" % lo] + ([] if b > 1 else ["rw%d" % (K - 1), "r16_3"]))
+                    c = c1
+            if k < KTOP:
                 gat2(into("f%d" % (k + 1)), fk, T.fw if k else T.hpw, K * k, r0 + (["fw%d" % k] if k else ["hpw"]), "f%d" % (k + 1), CUTS["ring"])
-        rws = ["rw%d" % j for j in range(6)]
-        v(lambda: V.tensor_copy(T.pmr[:, 0:449].indirect(T.rw[:, 0:K]), T.ids[:, 512:960]), rws + ["idz", "idc"], ["pmr"], L * 3)
         s = relay(T.pmr[:, 1:449], T.scr, "scr", ["pmr"])
         ts(T.pmw[:], s, cp, -512.0, ALU.mult, ALU.add, ["scr", "cp"], ["pmw"], K)
-        add(p, ("A",), lambda e: A.activation(T.m1[:], T.rrep[:], ACT.Copy, scale=1.0 / 1024), ["r16_%d" % k for k in range(3, 9)], ["m1"], L * CY)
-        tt(T.mono[:], T.m1[:], T.th0[:], ALU.add, ["m1", "th0"], ["mono"], 2 * L)
+
+        p["boost"] = 0.0
 
     gat2(into("mtr"), T.ids[:, 512:961], T.mtw, 0, ["mtw", "idc", "idz"], "mtr", 0)
-    RW = ["rw%d" % j for j in range(6)]
 
     def tn(i):
         return T.tiny[:, K * i:K * i + K]
@@ -470,40 +580,44 @@ def build(g, core, T, topo):
             ts(T.sgn[:, 1 + 224 * h:225 + 224 * h], T.pb[:, 512 * h:512 * h + 224], 0.0, 1.0, ALU.is_gt, ALU.add, [], ["bank%d" % (4 + h), "sgn%d" % h], 224)
         SG = ["sgn0", "sgn1"]
         gat(T.ga[:], T.sgn[:, 0:449], T["ivw%d" % m][:, 0:K], SG + ["sgni", "ivw%d" % m], ["ga"], L, ("V",))
-        gat(T.gb[:], T.sgn[:, 0:449], T["mvw%d" % m][:, 0:K], SG + ["sgni", "mvw%d" % m], ["gb"], L, ("A",))
+        add(p, ("A",), lambda e, m=m: A.activation(T.gb[:], T.sgn[:, 0:449].indirect(T["mvw%d" % m][:, 0:K]), ACT.Copy, bias=3.0, scale=-1.0),
+            SG + ["sgni", "mvw%d" % m], ["gb"], 0.055, ge=L)
         for a in "ab":
             v(lambda a=a: V.tensor_tensor_scan(T["y" + a][:], T.db[:], T["g" + a][:], 0.0, ALU.mult, ALU.max), ["db", "g" + a], ["y" + a], L // 2)
-        t1, t2, t3, t6, t7 = [tn(i) for i in (5, 6, 7, 8, 9)]
-        tt(t1, T.ya[:, 15:L:16], T.yb[:, 15:L:16], ALU.mult, ["ya", "yb"], ["t1"], 64)
-        ts(t2, t1, thr, None, ALU.is_ge, None, ["t1", "thr"], ["t2"], K)
+        t2, t3, t6, t7 = [tn(i) for i in (6, 7, 8, 9)]
+        tt(t2, T.ya[:, 15:L:16], T.yb[:, 15:L:16], ALU.is_gt, ["ya", "yb"], ["t2"], 64)
         tt(t3, t2, fl["dz%d" % m], ALU.mult, ["t2", "dz%d" % m], ["t3"], 64)
         tt(fl["z%d" % nx], t3, fl["z%d" % m], ALU.add, ["t3", "z%d" % m], ["z%d" % nx], 64)
         zo = T["zo%d" % m]
         ts(zo[:], fl["z%d" % nx], 512.0, None, ALU.mult, None, ["z%d" % nx], ["zo%d" % m], K)
+        p["tag"] = "iv%d" % m
         tt(t6, t2, fl["dm%d" % m], ALU.mult, ["t2", "dm%d" % m], ["t6"], 64)
         tt(fl["ivs%d" % nx], t6, fl["ivs%d" % m], ALU.add, ["t6", "ivs%d" % m], ["ivs%d" % nx], 64)
         ivw = T["ivw%d" % nx]
+        ts(ivw[:], fl["ivs%d" % nx], 512.0, None, ALU.mult, None, ["ivs%d" % nx], ["ivw%d" % nx], K)
+        send(dst, T["liv%d" % m][:], ivw[:], "ri%d" % m, ["ivw%d" % nx], [], 0, "out_i%d" % m)
+        arrive("ri%d" % m, n8, ["out_i%d" % m], ["liv%d" % m], 2.0)
+        p["tag"] = "sw%d" % m
         if nx < NR:
             ts(t7, t2, -2.0, 1.0, ALU.mult, ALU.add, ["t2"], ["t7"], K)
             for n in ("dm", "dz"):
                 tt(fl["%s%d" % (n, nx)], t7, fl["%s%d" % (n, m)], ALU.mult, ["t7", "%s%d" % (n, m)], ["%s%d" % (n, nx)], 64)
             tt(tn(10), fl["ivs%d" % nx], fl["dm%d" % nx], ALU.add, ["ivs%d" % nx, "dm%d" % nx], ["mvs"], 64)
             ts(T["mvw%d" % nx][:], tn(10), 512.0, None, ALU.mult, None, ["mvs"], ["mvw%d" % nx], K)
-        gat(T.gm[:], T.sgn[:, 0:449], T.mtw[:, 0:K], SG + ["sgni", "mtw"], ["gm"], L, ("A",))
+        p["tag"] = "ud%d" % m
+        add(p, ("A",), lambda e: A.activation(T.gm[:], T.sgn[:, 0:449].indirect(T.mtw[:, 0:K]), ACT.Copy, bias=3.0, scale=-1.0),
+            SG + ["sgni", "mtw"], ["gm"], 0.055, ge=L)
         v(lambda: V.tensor_tensor_scan(T.yc[:], T.db[:], T.sgn[:, 1:449], 0.0, ALU.mult, ALU.max), ["db"] + SG, ["yc"], L // 2)
         v(lambda: V.tensor_tensor_scan(T.yd[:], T.db[:], T.gm[:], 0.0, ALU.mult, ALU.max), ["db", "gm"], ["yd"], L // 2)
-        u1, u2, u3, u4 = [tn(i) for i in (11, 12, 13, 14)]
-        tt(u1, T.yc[:, 15:L:16], T.yd[:, 15:L:16], ALU.mult, ["yc", "yd"], ["u1"], 64)
-        ts(u2, u1, thr, None, ALU.is_ge, None, ["u1", "thr"], ["u2"], K)
+        u2, u3, u4 = [tn(i) for i in (12, 13, 14)]
+        tt(u2, T.yc[:, 15:L:16], T.yd[:, 15:L:16], ALU.is_gt, ["yc", "yd"], ["u2"], 64)
         tt(u3, u2, fl["dmu%d" % m], ALU.mult, ["u2", "dmu%d" % m], ["u3"], 64)
         tt(fl["uds%d" % nx], u3, fl["uds%d" % m], ALU.add, ["u3", "uds%d" % m], ["uds%d" % nx], 64)
         ts(T["udw%d" % m][:], fl["uds%d" % nx], 512.0, None, ALU.mult, None, ["uds%d" % nx], ["udw%d" % m], K)
         if nx < NR:
             ts(u4, u2, -2.0, 1.0, ALU.mult, ALU.add, ["u2"], ["u4"], K)
             tt(fl["dmu%d" % nx], u4, fl["dmu%d" % m], ALU.mult, ["u4", "dmu%d" % m], ["dmu%d" % nx], 64)
-        ts(ivw[:], fl["ivs%d" % nx], 512.0, None, ALU.mult, None, ["ivs%d" % nx], ["ivw%d" % nx], K)
-        send(dst, T["liv%d" % m][:], ivw[:], "ri%d" % m, ["ivw%d" % nx], [], 0, "out_i%d" % m)
-        arrive("ri%d" % m, n8, ["out_i%d" % m], ["liv%d" % m], 2.0)
+        p["tag"] = "up%d" % m
         first = min(m, 1)
         gat2(lambda a, b: T.w1[:, 513 + a:513 + b], T.ids[:, 0:961], zo, 0, ["idl", "idz", "idc", "zo%d" % m], "w1", CUTS["w"][first])
         gat2(into("p0"), T.w1[:, 0:961], zo, 0, ab("w1") + ["w1i", "zo%d" % m], "p0", CUTS["w"][first])
@@ -520,32 +634,42 @@ def build(g, core, T, topo):
         if m == 0:
             ring_ops()
         gat2(lambda a, b: T.vr[:, a:b], win(A_, 0, 450), T.rw, 0, ab(A_) + [A_ + "i", A_ + "j"] + RW, "vr", CUTS["r"])
-        v(lambda: V.tensor_tensor_scan(win("st", 1, 449), T.vr[:], T.mono[:], 512.0, ALU.max, ALU.min), ab("vr") + ["mono"], ["st"], L)
+        v(lambda: V.tensor_tensor_scan(win("st", 1, 449), T.vr[:], T.mono[:], 512.0, ALU.max, ALU.min), ab("vr") + MONO, ["st"], L)
         gat2(into("bwin"), win("st", 0, 449), T.pmw, 0, ["st", "sti", "pmw"], "bwin", CUTS["r"])
         s, sk = relay2("bwin", "sc", CUTS["r"] if SPLIT else 0)
         places(T.sc, sk, T["bw%d" % m], "bw%d" % m, 0)
         send(dst, T["lbw%d" % m][:], T["bw%d" % m][:], "rb%d" % m, ["bw%d" % m], [], 0, "out_b%d" % m)
         arrive("rb%d" % m, n8, ["out_b%d" % m], ["lbw%d" % m], 2.0)
+        p["tag"] = "e%d" % m
         gat2(lambda a, b: T.eb[:, a:b], win("bwin", 0, 449), T["liv%d" % m], 0, ab("bwin") + ["bwini", "liv%d" % m], "eb", 0)
         relay(T.eb[:], T.scb, "scb", ab("eb"))
         places(T.scb, ["scb"], T["ew%d" % m], "ew%d" % m, 1)
         send(dst, T["lew%d" % m][:], T["ew%d" % m][:], "re_%d" % m, ["ew%d" % m], [], 0, "out_e%d" % m)
         arrive("re_%d" % m, n8, ["out_e%d" % m], ["lew%d" % m], 2.0)
+        p["tag"] = "to%d" % m
         for b in range(4):
             mm(b, T.eqc, T.eqp, 128 * b, xc, xp, 0, L, X + ["eq%d" % b])
             unload(b, T.to[:, TW * b + 1:TW * b + 449], L, 1.0, ["to%d" % b])
+        p["tag"] = "tp%d" % m
         for b in range(4):
             mm(4 + b, T.eqc, T.eqp, 128 * b, lc, lp, 0, L, ["la%d" % m, "eq%d" % b])
             unload(4 + b, T.tp[:, TW * b + 1:TW * b + 449], L, 1.0, ["tp%d" % b])
+        p["tag"] = "ga%d" % m
         for b in range(4):
-            gat(T.g1[:, L * b:L * b + L], T.tp[:, TW * b:TW * b + 449], T["liv%d" % m][:, 0:K], ["tp%d" % b, "tpi%d" % b, "liv%d" % m], ["g1%d" % b], L, G1)
+            for c0, c1 in PARTS:
+                gat(T.g1[:, L * b + c0:L * b + c1], T.tp[:, TW * b:TW * b + 449], T["liv%d" % m][:, c0 // 16:c1 // 16],
+                    ["tp%d" % b, "tpi%d" % b, "liv%d" % m], ["g1%d_%d" % (b, c0)], c1 - c0, G1)
+        p["tag"] = "gb%d" % m
         for b in range(4):
-            gat(T.g2[:, L * b:L * b + L], T.to[:, TW * b:TW * b + 449], T["udw%d" % m][:, 0:K], ["to%d" % b, "toi%d" % b, "udw%d" % m], ["g2%d" % b], L)
+            for c0, c1 in PARTS:
+                gat(T.g2[:, L * b + c0:L * b + c1], T.to[:, TW * b:TW * b + 449], T["udw%d" % m][:, c0 // 16:c1 // 16],
+                    ["to%d" % b, "toi%d" % b, "udw%d" % m], ["g2%d_%d" % (b, c0)], c1 - c0)
+        p["tag"] = ""
         for h, (c0, c1) in enumerate(((0, CUT), (CUT, L))):
             for b in range(4):
                 v(lambda b=b, c0=c0, c1=c1, m=m: V.tensor_tensor(T.zt[:, 4 * c0 + b:4 * c1:4], T.tp[:, TW * b:TW * b + 449].indirect(T["lbw%d" % m][:, c0 // 16:c1 // 16]),
                                                                  T.g1[:, L * b + c0:L * b + c1], ALU.add),
-                  ["tp%d" % b, "tpi%d" % b, "lbw%d" % m, "g1%d" % b], ["zt%d%d" % (h, b)], 60 + (c1 - c0) * GC)
+                  ["tp%d" % b, "tpi%d" % b, "lbw%d" % m, "g1%d_%d" % (b, c0)], ["zt%d%d" % (h, b)], 60, c1 - c0)
             v(lambda c0=c0, c1=c1: V.quantize_mx(T.zqc[:, c0:c1], T.zqp[:, c0:c1], T.zt[:, 4 * c0:4 * c1]), ["zt%d%d" % (h, b) for b in range(4)], ["zq%d" % h], 14 + (c1 - c0) * 1.06)
             for b in range(4):
                 i = 4 * h + b
@@ -553,7 +677,7 @@ def build(g, core, T, topo):
                 unload(i, T.hh[:, TW * b + 1 + c0:TW * b + 1 + c1], c1 - c0, 0.015625, ["hh%d%d" % (b, h)])
         for b in range(4):
             v(lambda b=b, m=m: V.tensor_tensor(T.xnt[:, b:4 * L:4], T.hh[:, TW * b:TW * b + 449].indirect(T["lew%d" % m][:, 0:K]), T.g2[:, L * b:L * b + L], ALU.add),
-              ["hh%d0" % b, "hh%d1" % b, "hhi%d" % b, "lew%d" % m, "g2%d" % b], ["xnt%d" % b], 60 + L * GC)
+              ["hh%d0" % b, "hh%d1" % b, "hhi%d" % b, "lew%d" % m] + ["g2%d_%d" % (b, c0) for c0, c1 in PARTS], ["xnt%d" % b], 60, L)
         v(lambda nx=nx: V.quantize_mx(T["xqc%d" % nx][:], T["xqp%d" % nx][:], T.xnt[:]), ["xnt%d" % b for b in range(4)], ["xq%da" % nx, "xq%db" % nx], 14 + L * 1.06)
 
     outs = [0]
@@ -580,7 +704,7 @@ def rank_program(g, core, T, topo):
     if rank is None:
         return
     p, sent, outs, n8 = build(g, core, T, topo)
-    count, known, total = emit(g, T, p)
+    count = emit(g, T, p)
     for e, s in SEM.items():
         if count[e]:
             g.wait_ge(T.sem[s], count[e])

import numpy as np
from concourse.mybir import dt, AluOpType, ActivationFunctionType

ALU, ACT = AluOpType, ActivationFunctionType

L = 448
K = L // 16
NR = 3
STEP = [1, 2, 3]
CUT = 256
CUTS = {"ring": 0, "w": (0, 12), "b": (0, 14), "c": (0, 12), "r": 12}
PARTS = ((0, CUT), (CUT, L))
LV = 5
TW = 464

SCRATCH = {}


def _buf(name, cols, dtype="float32", where="sbuf"):
    SCRATCH[name] = (where, [128, cols], dtype)


for _n in ("l_iv", "l_hp", "l_mt", "l_ud"):
    _buf(_n, K, "int32")
_buf("x0t", 4 * L, "bfloat16")
_buf("ut", 512, "bfloat16")
_buf("vt", 512, "bfloat16")
_buf("zt", 4 * L, "bfloat16")
_buf("xnt", 4 * L, "bfloat16")
_buf("ebuf", 516, "bfloat16")
for _n, _c in (("uq", 128), ("uqs", 128), ("vq", 128), ("wq", 512), ("eq", 512), ("zq", L)):
    _buf(_n + "c", _c, "float8_e4m3fn_x4")
    _buf(_n + "p", _c, "uint8")
for _m in range(NR + 1):
    _buf("xqc%d" % _m, L, "float8_e4m3fn_x4")
    _buf("xqp%d" % _m, L, "uint8")
for _m in range(NR):
    _buf("lac%d" % _m, L, "float8_e4m3fn_x4")
    _buf("lap%d" % _m, L, "uint8")
    for _n in ("liv", "lbw", "lew", "bw", "ew"):
        _buf(_n + str(_m), K, "uint16")
    _buf("udw%d" % _m, K, "uint16")
    _buf("zo%d" % _m, K, "uint16")
for _m in range(NR + 1):
    _buf("ivw%d" % _m, K, "uint16")
    _buf("mvw%d" % _m, K, "uint16")
FLOATS = [_n + str(_m) for _m in range(NR + 1) for _n in ("ivs", "dm", "z", "dz", "uds", "dmu")]
_buf("lst", K * len(FLOATS))
_buf("udwi", K, "uint16")
_buf("hpw", K, "uint16")
_buf("mtw", K, "uint16")
_buf("rw", K, "uint16")
_buf("pmw", K, "uint16")
_buf("uoff", 8, "uint16")
_buf("uoi", 8, "int32")
_buf("o16", 16, "uint16")
_buf("ids", 961)
_buf("w1", 961)
FS, PS = 968, 456
WIN = {"f%d" % _k: ("fb", FS * _k) for _k in range(9)}
for _k, _n in enumerate(("p0", "p1", "p2", "st", "bwin", "mtr", "udrep")):
    WIN[_n] = ("wb", PS * _k)
_buf("fb", 9 * FS)
_buf("wb", 7 * PS)
_buf("fw", 8 * K + 32, "uint16")
_buf("offw", 8 * K, "uint16")
_buf("sgn", 449, "bfloat16")
for _n in ("ga", "gb", "gm", "ya", "yb", "yc", "yd", "db"):
    _buf(_n, L, "bfloat16")
for _n in ("d2", "sc", "scb", "scm", "scu", "scr", "tmod", "th0", "rrep", "mono", "m1", "vr", "eb", "mv", "um", "ysb", "uf", "uf0", "s16", "g16"):
    _buf(_n, L)
_buf("pmr", 449)
_buf("cidx", K)
_buf("jws", K)
_buf("tiny", 15 * K)
_buf("ti", 4 * K, "int32")
_buf("pcol", 8, "int32")
_buf("col", 16)
_buf("ones", 16)
_buf("half", 16)
_buf("cps", 16)
_buf("to", 4 * TW, "bfloat16")
_buf("tp", 4 * TW, "bfloat16")
_buf("hh", 4 * TW, "bfloat16")
_buf("g1", 4 * L, "bfloat16")
_buf("g2", 4 * L, "bfloat16")
_buf("pa", 2048, "float32", "psum")
_buf("pb", 2048, "float32", "psum")

LOADS = ["d_hp", "d_iv", "d_mt", "d_ud", "d_u", "d_xa", "d_xb", "d_v", "d_wc", "d_ws"]
SEMAPHORES = ["sv", "sa", "sp", "sg", "sent", "d_out"] + LOADS + ["%s%d" % (a, m) for a in ("rc", "ri", "rb", "re_") for m in range(NR)]
SEM = {"V": "sv", "A": "sa", "P": "sp", "G": "sg"}
CY = 0.00083
DELTA = 0.12
AHEAD = 0.8
G1 = ("V", "A")
SPLIT = True
KTOP = 6
BOOST = (30.0, 0.0)


def new_prog():
    return {"ops": [], "wr": {}, "rd": {}, "boost": 0.0, "tag": ""}


def add(p, eng, fn, r, w, dur, lat=0.0, kind="c", sem=None, val=1, ge=0):
    ops = p["ops"]
    i = len(ops)
    deps = set()
    for k in r:
        if k in p["wr"]:
            deps.add(p["wr"][k])
        else:
            raise ValueError("read before write: " + k)
    for k in w:
        if k in p["wr"]:
            deps.add(p["wr"][k])
        for j in p["rd"].get(k, ()):
            deps.add(j)
    for k in r:
        p["rd"].setdefault(k, []).append(i)
    for k in w:
        p["wr"][k] = i
        p["rd"][k] = []
    deps.discard(i)
    ops.append({"boost": p["boost"], "tag": p["tag"], "eng": eng, "fn": fn, "deps": sorted(deps), "dur": dur, "ge": ge, "lat": lat, "kind": kind, "sem": sem, "val": val})
    return i


MOVES = 16000
COSTS = [(1.5, 1.2, 0.08, 1.0), (1.1, 1.1, 0.05, 1.4), (2.0, 1.3, 0.12, 0.8)]
LIFT = {"iv": 8.0, "tp": 3.0, "ga": 3.0, "ud": 3.0}
FOUND = {}


def order(ops):
    key = (len(ops), sum(len(o["deps"]) for o in ops))
    if key not in FOUND:
        FOUND[key] = better(ops, *schedule(ops))
    return FOUND[key]


def cost(o, c):
    return (o["dur"] + o["ge"] * c[0] * CY) * c[1]


def walk(ops, seq, on, c, durs, paths):
    free, end, before, why = {}, [0.0] * len(ops), {}, {}
    wake, late = c[2], c[3]
    for i in seq:
        o = ops[i]
        t, b = 0.0, None
        for d in o["deps"]:
            x = end[d] + wake
            if x > t:
                t, b = x, (d, False)
        e, k = on[i], durs[i]
        if e != "N":
            f = free.get(e, 0.0)
            if f > t:
                t, b = f, (before[e], True)
            free[e] = t + k
            before[e] = i
        end[i] = t + k + o["lat"] * late
        if paths:
            why[i] = b
    if not paths:
        return max(end)
    i = max(seq, key=lambda i: end[i])
    found = []
    while why[i] is not None:
        if why[i][1]:
            found.append((i, why[i][0]))
        i = why[i][0]
    return found


def better(ops, seq, on):
    n = len(ops)
    rng = np.random.RandomState(3)
    succ = [[] for _ in range(n)]
    for i, o in enumerate(ops):
        for d in o["deps"]:
            succ[d].append(i)
    durs = [[cost(o, c) for o in ops] for c in COSTS]

    def total(s, o):
        return sum(walk(ops, s, o, c, k, False) for c, k in zip(COSTS, durs))
    now = total(seq, on)
    best, path = (now, seq, on), None
    dice = rng.random_sample((MOVES, 6)).tolist()
    for k in range(MOVES):
        r = dice[k]
        if path is None or k % 15 == 0:
            c = int(r[5] * len(COSTS))
            path = walk(ops, seq, on, COSTS[c], durs[c], True)
        if not path:
            continue
        i, j = path[int(r[0] * len(path))]
        seq2, on2 = seq, on
        flex = [x for x in (i, j) if len(ops[x]["eng"]) > 1]
        if r[1] < 0.15 and flex:
            x = flex[int(r[2] * len(flex))]
            on2 = list(on)
            on2[x] = "A" if on[x] == "V" else "V"
        else:
            pi, pj = seq.index(i), seq.index(j)
            if pi < pj:
                continue
            far = int(r[3] * 60) if r[4] < 0.4 else 0
            if r[1] < 0.6:
                needs = set(succ[j])
                to = pi + 1
                if any(x in needs for x in seq[pj + 1:to]):
                    continue
                while far and to < n and seq[to] not in needs:
                    to, far = to + 1, far - 1
                seq2 = seq[:pj] + seq[pj + 1:to] + [j] + seq[to:]
            else:
                needs = set(ops[i]["deps"])
                to = pj
                if any(x in needs for x in seq[to:pi]):
                    continue
                while far and to > 0 and seq[to - 1] not in needs:
                    to, far = to - 1, far - 1
                seq2 = seq[:to] + [i] + seq[to:pi] + seq[pi + 1:]
        t = total(seq2, on2)
        if t <= now + 0.25 * (1 - k / MOVES) * r[2] ** 2:
            if t != now:
                path = None
            seq, on, now = seq2, on2, t
            if t < best[0] - 1e-9:
                best = (t, seq, on)
    return best[1], best[2]


def schedule(ops):
    n = len(ops)
    WAKE = COSTS[0][2]
    dur = [cost(o, COSTS[0]) for o in ops]
    succ = [[] for _ in range(n)]
    for i, o in enumerate(ops):
        for d in o["deps"]:
            succ[d].append(i)
    prio = [0.0] * n
    for i in range(n - 1, -1, -1):
        prio[i] = dur[i] + ops[i]["lat"] + WAKE + max([prio[s] for s in succ[i]] + [0.0])
    free, left = {}, [len(o["deps"]) for o in ops]
    end, when, on = [0.0] * n, [0.0] * n, [None] * n
    ready = {i: 0.0 for i in range(n) if not left[i]}
    while ready:
        cand = []
        for i, at in ready.items():
            for e in ops[i]["eng"]:
                f = free.get(e, 0.0)
                cand.append((at if at > f else f, i, e))
        first = min(cand)
        t0 = first[0]
        late = t0 + max(DELTA, AHEAD * dur[first[1]])
        t, i, e = max([c for c in cand if c[2] == first[2] and c[0] <= late], key=lambda c: (prio[c[1]] - (c[0] - t0), -c[1]))
        o = ops[i]
        del ready[i]
        when[i], on[i] = t, e
        if e != "N":
            free[e] = t + dur[i]
        end[i] = t + dur[i] + o["lat"]
        for s in succ[i]:
            left[s] -= 1
            if not left[s]:
                ready[s] = max(end[d] + WAKE for d in ops[s]["deps"])
    return sorted(range(n), key=lambda i: (when[i], i)), on


def emit(g, T, p):
    ops = p["ops"]
    seq, on = order(ops)
    when = {i: k for k, i in enumerate(seq)}
    q = {"V": g.vector, "A": g.scalar, "P": g.tensor, "G": g, "S": g.sync}
    count = {e: 0 for e in q}
    known = {e: {} for e in q}
    clock = [None] * len(ops)
    for i in seq:
        o, e = ops[i], on[i]
        if e == "N":
            clock[i] = {o["sem"]: o["val"]}
            continue
        need = {}
        for d in o["deps"]:
            if ops[d]["kind"] == "r":
                continue
            for s, v in clock[d].items():
                need[s] = max(need.get(s, 0), v)
        mine = known[e]
        direct = []
        for d in sorted(o["deps"], key=lambda d: -when[d]):
            if ops[d]["kind"] == "r":
                continue
            s, v = own(ops, on, clock, d)
            if mine.get(s, 0) < v:
                q[e].wait_ge(T.sem[s], v)
                for s2, v2 in clock[d].items():
                    if mine.get(s2, 0) < v2:
                        mine[s2] = v2
        inst = o["fn"](e)
        c = dict(mine)
        if o["kind"] == "c":
            count[e] += 1
            inst.then_inc(T.sem[SEM[e]], 1)
            c[SEM[e]] = count[e]
        elif o["kind"] == "d":
            inst.then_inc(T.sem[o["sem"]], 16)
            c[o["sem"]] = 16
        clock[i] = c
        ops[i]["n"] = count[e]
    return count


def own(ops, on, clock, d):
    o = ops[d]
    if o["kind"] == "c":
        return SEM[on[d]], o["n"]
    return o["sem"], (16 if o["kind"] == "d" else o["val"])


def build(g, core, T, topo):
    rank = T.rank_of(core)
    p = new_prog()
    V, A, P, G = g.vector, g.scalar, g.tensor, g
    U8, U32 = dt.uint8, dt.uint32

    def v(fn, r, w, el, ge=0):
        return add(p, ("V",), lambda e: fn(), r, w, (el if ge else max(64, el)) * CY, ge=ge)

    def ts(out, in0, s1, s2, op0, op1, r, w, el):
        if op1 is None:
            return v(lambda: V.tensor_scalar(out, in0, s1, None, op0), r, w, el)
        return v(lambda: V.tensor_scalar(out, in0, s1, s2, op0, op1), r, w, el)

    def tt(out, a, b, op, r, w, el):
        return v(lambda: V.tensor_tensor(out, a, b, op), r, w, el)

    def fill(ap, c, w, el):
        return v(lambda: V.memset(ap, c), [], w, el)

    def gat(out, win, off, r, w, el, eng=("V", "A")):
        def fn(e):
            if e == "V":
                return V.tensor_copy(out, win.indirect(off))
            return A.activation(out, win.indirect(off), ACT.Copy)
        return add(p, eng, fn, r, w, 0.055, ge=el)

    def win(n, a, b):
        t, o = WIN[n]
        return T[t][:, o + a:o + b]

    def gat2(out, window, off, oo, r, key, cut):
        h = 16 * cut
        if cut in (-1, 0, K):
            gat(out(0, L), window, off[:, oo:oo + K], r, [key + "a", key + "b"], L, ("V", "A") if cut < 0 else ("A",) if cut == 0 else ("V",))
            return
        gat(out(0, h), window, off[:, oo:oo + cut], r, [key + "a"], h, ("V",))
        gat(out(h, L), window, off[:, oo + cut:oo + K], r, [key + "b"], L - h, ("A",))

    def into(n):
        return lambda a, b: win(n, 1 + a, 1 + b)

    def ab(k):
        return [k + "a", k + "b"]

    def relay(src, sc, sck, r, n=L):
        v(lambda: V.tensor_tensor_scan(sc[:, 0:n], T.d2[:, 0:n], src, 0.0, ALU.mult, ALU.max), r + ["d2"], [sck], n)
        return sc[:, 15:n:16]

    def relay2(key, sck, cut):
        h = 16 * cut
        if cut in (-1, 0, K):
            return relay(win(key, 1, 1 + L), T.sc, sck + "b", ab(key)), [sck + "b"]
        for a, b, c in ((0, h, "a"), (h, L, "b")):
            v(lambda a=a, b=b: V.tensor_tensor_scan(T.sc[:, a:b], T.d2[:, a:b], win(key, 1 + a, 1 + b), 0.0, ALU.mult, ALU.max), [key + c, "d2"], [sck + c], b - a)
        return T.sc[:, 15:L:16], ab(sck)

    cp = T.cps[:, 15:16]
    cpk, kf = T.col[:, 1:2], T.col[:, 4:5]
    bias = [T.col[:, 8 + k:9 + k] for k in range(4)]
    idc = T.ids[:, 513:961]
    fl = {n: T.lst[:, K * i:K * i + K] for i, n in enumerate(FLOATS)}

    def load(q, out, in_, sem, w, lat, r=()):
        add(p, (q,), lambda e: (g.sync if e == "S" else g.scalar).dma_start(out, in_), list(r), w, 0.05, lat, "d", sem)
    load("S", T.l_hp[:], T.hp[:], "d_hp", ["l_hp"], 2.0)
    load("A", T.l_iv[:], T.iv[:], "d_iv", ["l_iv"], 2.0)
    load("A", T.l_mt[:], T.mt[:], "d_mt", ["l_mt"], 2.0)
    load("A", T.l_ud[:], T.ud[:], "d_ud", ["l_ud"], 2.0)
    load("S", T.ut[:], T.u[:], "d_u", ["ut"], 2.5)
    load("S", T.x0t[:, 0:4 * CUT], T.x[:, 0:4 * CUT], "d_xa", ["x0a"], 3.5)
    load("S", T.x0t[:, 4 * CUT:4 * L], T.x[:, 4 * CUT:4 * L], "d_xb", ["x0b"], 4.0)
    load("S", T.wqc[:].bitcast(U8), T.wc[:], "d_wc", ["wqc"], 4.0, ["x0b"])
    load("S", T.wqp[:], T.ws[:], "d_ws", ["wqp"], 3.0, ["x0b"])
    load("S", T.vt[:], T.v[:], "d_v", ["vt"], 3.0, ["x0b"])

    def iota(out, pat, base, cm, w, el, flag=True):
        if flag:
            fn = lambda e: G.iota(out, pat, base, cm, allow_small_or_imprecise_dtypes=True)
        else:
            fn = lambda e: G.iota(out, pat, base, cm)
        add(p, ("G",), fn, [], w, 0.13 + 2 * el * CY)
    iota(T.pcol[:, 0:1], [[0, 1]], 0, 1, ["pcol"], 1, False)
    iota(T.tmod[:], [[0, K], [1, 16]], 0, 0, ["tmod"], L)
    iota(idc, [[1, L]], 513, 0, ["idc"], L)
    iota(T.cidx[:], [[16, K]], 1, 0, ["cidx"], K)
    iota(T.uoi[:], [[16, 8]], 0, 0, ["uoi"], 8, False)
    for k in range(4):
        iota(win("f%d" % k, 449, 961), [[1, 512]], 449, 0, ["f%dI" % k], 512)
    fill(T.ebuf[:], 0.5, ["ebuf0"], 258)
    add(p, ("G",), lambda e: G.affine_select(T.ebuf[:], T.ebuf[:], [[-1, 516]], ALU.is_equal, 0.0, 3, 4), ["ebuf0"], ["ebuf"], 0.17 + 2 * 516 * CY)
    fill(T.ones[:], 1.0, ["ones"], 16)
    ts(T.pcol[:, 1:2], T.pcol[:, 0:1], 15, None, ALU.bitwise_and, None, ["pcol"], ["kint"], 1)
    v(lambda: V.tensor_copy(kf, T.pcol[:, 1:2]), ["kint"], ["kf"], 1)
    ts(T.d2[:], T.tmod[:], kf, 2.0, ALU.is_gt, ALU.mult, ["tmod", "kf"], ["d2"], L)
    ts(T.half[:], T.d2[:, 0:16], -0.25, 1.0, ALU.mult, ALU.add, ["d2"], ["half"], 16)
    v(lambda: V.tensor_tensor_scan(T.cps[:], T.half[:], T.ones[:], 1.0, ALU.mult, ALU.min), ["half", "ones"], ["cp"], 16)
    ts(cpk, cp, 1.0 / 512, None, ALU.mult, None, ["cp"], ["cpk"], 1)
    for k in range(4):
        ts(T.pcol[:, 2 + k:3 + k], T.pcol[:, 0:1], 1 << k, None, ALU.bitwise_and, None, ["pcol"], ["bit%d" % k], 1)
        ts(bias[k], T.pcol[:, 2 + k:3 + k], 512.0 / (1 << k), -512.0, ALU.mult, ALU.add, ["bit%d" % k], ["bias%d" % k], 1)
    fill(T.o16[:, 8:9], 448, ["o16_s"], 1)
    fill(T.ids[:, 0:512], 512.0, ["idl"], 512)
    fill(T.ids[:, 512:513], 960.0, ["idz"], 1)
    fill(T.fb[:, 0:8 * FS + 1:FS], 512.0, ["f%di" % k for k in range(9)], 9)
    fill(T.wb[:, 0:6 * PS + 1:PS], 512.0, ["p0i", "p1i", "p2i", "sti", "bwini", "mtri", "udrepi"], 7)
    fill(T.wb[:, 449:449 + 2 * PS + 1:PS], 961.0, ["p0j", "p1j", "p2j"], 3)
    fill(T.sgn[:, 0:1], 1.0, ["sgni"], 1)
    fill(T.w1[:, 0:513], 961.0, ["w1i"], 513)
    for n in ("to", "tp", "hh"):
        fill(T[n][:, 0:3 * TW + 1:TW], 0.0, ["%si%d" % (n, b) for b in range(4)], 4)
    add(p, ("A",), lambda e: A.activation(T.db[:], T.d2[:], ACT.Copy), ["d2"], ["db"], L * CY)
    ts(T.jws[:], T.cidx[:], kf, 1.0 / 512, ALU.add, ALU.mult, ["cidx", "kf"], ["jws"], K)
    add(p, ("V", "A"), lambda e: V.tensor_scalar(T.th0[:], idc, 0.5, 255.0, ALU.mult, ALU.add) if e == "V" else
        A.activation(T.th0[:], idc, ACT.Copy, bias=255.0, scale=0.5), ["idc"], ["th0"], L * CY)
    v(lambda: V.tensor_copy(T.uoff[:], T.uoi[:]), ["uoi"], ["uoff"], 8)

    p["boost"] = BOOST[0]
    ts(T.hpw[:], T.l_hp[:], 1.0, None, ALU.add, None, ["l_hp"], ["hpw"], K)
    p["boost"] = 0.0
    ts(T.ivw0[:], T.l_iv[:], 1.0, None, ALU.add, None, ["l_iv"], ["ivw0"], K)
    ts(fl["ivs0"], T.l_iv[:], 1.0 / 512, 1.0 / 512, ALU.mult, ALU.add, ["l_iv"], ["ivs0"], K)
    ts(T.udwi[:], T.l_ud[:], 1.0, None, ALU.add, None, ["l_ud"], ["udwi"], K)
    ts(fl["uds0"], T.l_ud[:], 1.0 / 512, 1.0 / 512, ALU.mult, ALU.add, ["l_ud"], ["uds0"], K)
    ts(T.mtw[:], T.l_mt[:], 1.0, None, ALU.add, None, ["l_mt"], ["mtw"], K)

    v(lambda: V.quantize_mx(T.uqc[:, 0:128], T.uqp[:, 0:128], T.ut[:]), ["ut"], ["uq"], 140)
    v(lambda: V.tensor_copy(T.uqsc[:, 0:128].bitcast(U32), T.uqc[:, 0:128].bitcast(U32).indirect(T.uoff[:, 0:8])), ["uq", "uoff"], ["uqsc"], 200)
    add(p, ("A",), lambda e: A.activation(T.uqsp[:, 0:128], T.uqp[:, 0:128].indirect(T.uoff[:, 0:8]), ACT.Copy), ["uq", "uoff"], ["uqsp"], 200 * CY)
    for h, (a, b) in enumerate(((0, CUT), (CUT, L))):
        v(lambda a=a, b=b: V.quantize_mx(T.xqc0[:, a:b], T.xqp0[:, a:b], T.x0t[:, 4 * a:4 * b]), ["x0" + "ab"[h]], ["xq0" + "ab"[h]], (b - a) * 1.06 + 14)
    for b in range(4):
        v(lambda b=b: V.quantize_mx(T.eqc[:, 128 * b:128 * b + 128], T.eqp[:, 128 * b:128 * b + 128], T.ebuf[:, 3 - b:515 - b]), ["ebuf"], ["eq%d" % b], 150)

    def send(dst, out, in_, sem, r, w, lat, key):
        rid, pid = topo.addr(dst)[:2]
        add(p, ("G",), lambda e: g.remote_dma(out, in_, T.sem[sem], T.sem.sent, pid, rid, topo.mask(core, dst)), r, [key], 0.3, 0.0, "r")
        sent[0] += len(topo.engines(core, dst))

    sent = [0]

    def arrive(sem, val, r, w, lat):
        add(p, ("N",), None, r, w, 0.0, lat, "n", sem, val)

    RW, MONO = [], []

    def ring_ops():
        p["boost"] = BOOST[1]
        gat2(into("f0"), T.ids[:, 512:961], T.hpw, 0, ["hpw", "idc", "idz"], "f0", 0)
        gat(T.g16[:, 64:80], win("f0", 0, 449), T.o16[:, 8:9], ab("f0") + ["f0i", "o16_s"], ["r16_s"], 32, ("V",))
        ts(T.o16[:, 0:1], T.g16[:, 64:65], bias[0], None, ALU.add, None, ["r16_s", "bias0"], ["o16_0"], 1)

        def piece(lo, hi, r):
            a, b = 16 * lo, 16 * hi
            v(lambda: V.tensor_copy(T.pmr[:, 0:449].indirect(T.rw[:, lo:hi]), T.ids[:, 512 + a:512 + b]), r + ["idz", "idc"], ["pmr"], 60 + (b - a) * 3)
            add(p, ("V", "A"), lambda e: A.activation(T.m1[:, a:b], T.rrep[:, a:b], ACT.Copy, scale=1.0 / 1024) if e == "A" else
                V.tensor_scalar(T.m1[:, a:b], T.rrep[:, a:b], 1.0 / 1024, None, ALU.mult), r, ["m1_%d" % lo], max(64, b - a) * CY)
            tt(T.mono[:, a:b], T.m1[:, a:b], T.th0[:, a:b], ALU.add, ["m1_%d" % lo, "th0"], ["mono%d" % lo], 2 * (b - a))
            MONO.append("mono%d" % lo)

        for k in range(KTOP + 1):
            fk = win("f%d" % k, 0, 449)
            if 0 < k < KTOP:
                s = relay(win("f%d" % k, 1, 449), T.scr, "scr", ab("f%d" % k))
                ts(T.fw[:, K * k:K * k + K], s, cp, -512.0, ALU.mult, ALU.add, ["scr", "cp"], ["fw%d" % k], K)
            r0 = ab("f%d" % k) + ["f%di" % k]
            if k < 4:
                o = T.rrep[:, L - 16:L] if k == 3 else T.g16[:, 16 * k:16 * k + 16]
                gat(o, win("f%d" % k, 0, 961), T.o16[:, 2 * k:2 * k + 1], r0 + ["f%dI" % k, "o16_%d" % k], ["r16_%d" % k], 32, ("V",))
                s = relay(o, T.s16, "s16", ["r16_%d" % k], 16)
                if k < 3:
                    ts(T.o16[:, 2 * k + 2:2 * k + 3], s, cp, bias[k + 1], ALU.mult, ALU.add, ["s16", "cp", "bias%d" % (k + 1)], ["o16_%d" % (k + 1)], 1)
                else:
                    ts(T.o16[:, 10:11], s, cp, -512.0, ALU.mult, ALU.add, ["s16", "cp"], ["rwx"], 1)
                    ts(T.rw[:, K - 1:K], s, cp, -512.0, ALU.mult, ALU.add, ["s16", "cp"], ["rw%d" % (K - 1)], 1)
                    RW.append("rw%d" % (K - 1))
            else:
                b = 1 << (k - 4)
                c = b
                while c < K and (c == b or k == KTOP):
                    c1 = min(c + b, K)
                    lo, hi = K - c1, K - c
                    blk = 16 * (hi - lo)
                    if b == 1:
                        gat(T.rrep[:, 16 * lo:16 * hi], fk, T.o16[:, 10:11], r0 + ["rwx"], ["rr%d" % lo], 16, ("V",))
                    else:
                        gat(T.rrep[:, 16 * lo:16 * hi], fk, T.rw[:, lo + b:hi + b], r0 + [x for x in RW if lo + b <= int(x[2:]) < hi + b], ["rr%d" % lo], blk)
                    s = relay(T.rrep[:, 16 * lo:16 * hi], T.s16, "s16", ["rr%d" % lo], blk)
                    ts(T.rw[:, lo:hi], s, cp, -512.0, ALU.mult, ALU.add, ["s16", "cp"], ["rw%d" % lo], hi - lo)
                    RW.append("rw%d" % lo)
                    piece(lo, hi if b > 1 else K, ["rw%d" % lo, "rr%d" % lo] + ([] if b > 1 else ["rw%d" % (K - 1), "r16_3"]))
                    c = c1
            if k < KTOP:
                gat2(into("f%d" % (k + 1)), fk, T.fw if k else T.hpw, K * k, r0 + (["fw%d" % k] if k else ["hpw"]), "f%d" % (k + 1), CUTS["ring"])
        s = relay(T.pmr[:, 1:449], T.scr, "scr", ["pmr"])
        ts(T.pmw[:], s, cp, -512.0, ALU.mult, ALU.add, ["scr", "cp"], ["pmw"], K)

        p["boost"] = 0.0

    gat2(into("mtr"), T.ids[:, 512:961], T.mtw, 0, ["mtw", "idc", "idz"], "mtr", 0)

    def tn(i):
        return T.tiny[:, K * i:K * i + K]

    gat2(lambda a, b: T.mv[:, a:b], win("mtr", 0, 449), T.ivw0, 0, ab("mtr") + ["mtri", "ivw0"], "mv", 0)
    s = relay(T.mv[:], T.scm, "scm", ab("mv"))
    ts(T.mvw0[:], s, cp, -512.0, ALU.mult, ALU.add, ["scm", "cp"], ["mvw0"], K)
    ts(tn(0), s, cpk, -1.0, ALU.mult, ALU.add, ["scm", "cpk"], ["mvs0"], K)
    tt(fl["dm0"], tn(0), fl["ivs0"], ALU.subtract, ["mvs0", "ivs0"], ["dm0"], 64)
    tt(tn(1), tn(0), T.jws[:], ALU.is_gt, ["mvs0", "jws"], ["zm0"], 64)
    tt(tn(2), tn(0), tn(1), ALU.add, ["mvs0", "zm0"], ["zm1"], 64)
    tt(tn(3), fl["ivs0"], T.jws[:], ALU.is_gt, ["ivs0", "jws"], ["zi0"], 64)
    tt(fl["z0"], fl["ivs0"], tn(3), ALU.add, ["ivs0", "zi0"], ["z0"], 64)
    tt(fl["dz0"], tn(2), fl["z0"], ALU.subtract, ["zm1", "z0"], ["dz0"], 64)
    gat2(into("udrep"), T.ids[:, 512:961], T.udwi, 0, ["udwi", "idc", "idz"], "udrep", 0)
    gat2(lambda a, b: T.um[:, a:b], win("udrep", 0, 449), T.mtw, 0, ab("udrep") + ["udrepi", "mtw"], "um", 0)
    s = relay(T.um[:], T.scu, "scu", ab("um"))
    ts(tn(4), s, cpk, -1.0, ALU.mult, ALU.add, ["scu", "cpk"], ["mus"], K)
    tt(fl["dmu0"], tn(4), fl["uds0"], ALU.subtract, ["mus", "uds0"], ["dmu0"], 64)

    def places(sc, sck, out, key, i):
        t = T.ti
        ts(t[:, 2 * K * i:2 * K * i + K], sc[:, 15:L:16], cp, 1024.0, ALU.mult, ALU.mult, sck + ["cp"], ["ti%da" % i], K)
        ts(t[:, 2 * K * i + K:2 * K * i + 2 * K], t[:, 2 * K * i:2 * K * i + K], 511, None, ALU.bitwise_and, None, ["ti%da" % i], ["ti%db" % i], K)
        v(lambda: V.tensor_copy(out[:], t[:, 2 * K * i + K:2 * K * i + 2 * K]), ["ti%db" % i], [key], K)

    def bank(i):
        t = (T.pa, T.pb)[i // 4]
        return t, 512 * (i % 4)

    def mm(i, wc, wp, a, xc, xp, c0, c1, r):
        t, o = bank(i)
        add(p, ("P",), lambda e: P.matmul_mx(t[:, o:o + c1 - c0], wc[:, a:a + 128], wp[:, a:a + 128], xc[:, c0:c1], xp[:, c0:c1], True, True),
            r, ["bank%d" % i], (c1 - c0 + 16) * CY)

    def unload(i, out, n, scale, w):
        t, o = bank(i)

        def fn(e):
            if e == "A":
                return A.activation(out, t[:, o:o + n], ACT.Copy) if scale == 1.0 else A.activation(out, t[:, o:o + n], ACT.Copy, scale=scale)
            return V.tensor_copy(out, t[:, o:o + n]) if scale == 1.0 else V.tensor_scalar(out, t[:, o:o + n], scale, None, ALU.mult)
        add(p, ("V", "A"), fn, [], ["bank%d" % i] + w, 0.02 + n * CY)

    for m in range(NR):
        dst = T.cores[rank ^ STEP[m]]
        n8 = len(topo.engines(core, dst))
        X = ["xq%da" % m, "xq%db" % m]
        xc, xp, lc, lp = T["xqc%d" % m], T["xqp%d" % m], T["lac%d" % m], T["lap%d" % m]
        nx = m + 1
        send(dst, lc[:].bitcast(U8), xc[:].bitcast(U8), "rc%d" % m, X, [], 0, "out_c%d" % m)
        send(dst, lp[:], xp[:], "rc%d" % m, X, [], 0, "out_s%d" % m)
        arrive("rc%d" % m, 2 * n8, ["out_c%d" % m, "out_s%d" % m], ["la%d" % m], 6.0)
        for h in (0, 1):
            mm(4 + h, T.uqsc, T.uqsp, 0, xc, xp, 224 * h, 224 * h + 224, X + ["uqsc", "uqsp"])
            ts(T.sgn[:, 1 + 224 * h:225 + 224 * h], T.pb[:, 512 * h:512 * h + 224], 0.0, 1.0, ALU.is_gt, ALU.add, [], ["bank%d" % (4 + h), "sgn%d" % h], 224)
        SG = ["sgn0", "sgn1"]
        gat(T.ga[:], T.sgn[:, 0:449], T["ivw%d" % m][:, 0:K], SG + ["sgni", "ivw%d" % m], ["ga"], L, ("V",))
        add(p, ("A",), lambda e, m=m: A.activation(T.gb[:], T.sgn[:, 0:449].indirect(T["mvw%d" % m][:, 0:K]), ACT.Copy, bias=3.0, scale=-1.0),
            SG + ["sgni", "mvw%d" % m], ["gb"], 0.055, ge=L)
        for a in "ab":
            v(lambda a=a: V.tensor_tensor_scan(T["y" + a][:], T.db[:], T["g" + a][:], 0.0, ALU.mult, ALU.max), ["db", "g" + a], ["y" + a], L // 2)
        t2, t3, t6, t7 = [tn(i) for i in (6, 7, 8, 9)]
        tt(t2, T.ya[:, 15:L:16], T.yb[:, 15:L:16], ALU.is_gt, ["ya", "yb"], ["t2"], 64)
        tt(t3, t2, fl["dz%d" % m], ALU.mult, ["t2", "dz%d" % m], ["t3"], 64)
        tt(fl["z%d" % nx], t3, fl["z%d" % m], ALU.add, ["t3", "z%d" % m], ["z%d" % nx], 64)
        zo = T["zo%d" % m]
        ts(zo[:], fl["z%d" % nx], 512.0, None, ALU.mult, None, ["z%d" % nx], ["zo%d" % m], K)
        p["tag"] = "iv%d" % m
        tt(t6, t2, fl["dm%d" % m], ALU.mult, ["t2", "dm%d" % m], ["t6"], 64)
        tt(fl["ivs%d" % nx], t6, fl["ivs%d" % m], ALU.add, ["t6", "ivs%d" % m], ["ivs%d" % nx], 64)
        ivw = T["ivw%d" % nx]
        ts(ivw[:], fl["ivs%d" % nx], 512.0, None, ALU.mult, None, ["ivs%d" % nx], ["ivw%d" % nx], K)
        send(dst, T["liv%d" % m][:], ivw[:], "ri%d" % m, ["ivw%d" % nx], [], 0, "out_i%d" % m)
        arrive("ri%d" % m, n8, ["out_i%d" % m], ["liv%d" % m], 2.0)
        p["tag"] = "sw%d" % m
        if nx < NR:
            ts(t7, t2, -2.0, 1.0, ALU.mult, ALU.add, ["t2"], ["t7"], K)
            for n in ("dm", "dz"):
                tt(fl["%s%d" % (n, nx)], t7, fl["%s%d" % (n, m)], ALU.mult, ["t7", "%s%d" % (n, m)], ["%s%d" % (n, nx)], 64)
            tt(tn(10), fl["ivs%d" % nx], fl["dm%d" % nx], ALU.add, ["ivs%d" % nx, "dm%d" % nx], ["mvs"], 64)
            ts(T["mvw%d" % nx][:], tn(10), 512.0, None, ALU.mult, None, ["mvs"], ["mvw%d" % nx], K)
        p["tag"] = "ud%d" % m
        add(p, ("A",), lambda e: A.activation(T.gm[:], T.sgn[:, 0:449].indirect(T.mtw[:, 0:K]), ACT.Copy, bias=3.0, scale=-1.0),
            SG + ["sgni", "mtw"], ["gm"], 0.055, ge=L)
        v(lambda: V.tensor_tensor_scan(T.yc[:], T.db[:], T.sgn[:, 1:449], 0.0, ALU.mult, ALU.max), ["db"] + SG, ["yc"], L // 2)
        v(lambda: V.tensor_tensor_scan(T.yd[:], T.db[:], T.gm[:], 0.0, ALU.mult, ALU.max), ["db", "gm"], ["yd"], L // 2)
        u2, u3, u4 = [tn(i) for i in (12, 13, 14)]
        tt(u2, T.yc[:, 15:L:16], T.yd[:, 15:L:16], ALU.is_gt, ["yc", "yd"], ["u2"], 64)
        tt(u3, u2, fl["dmu%d" % m], ALU.mult, ["u2", "dmu%d" % m], ["u3"], 64)
        tt(fl["uds%d" % nx], u3, fl["uds%d" % m], ALU.add, ["u3", "uds%d" % m], ["uds%d" % nx], 64)
        ts(T["udw%d" % m][:], fl["uds%d" % nx], 512.0, None, ALU.mult, None, ["uds%d" % nx], ["udw%d" % m], K)
        if nx < NR:
            ts(u4, u2, -2.0, 1.0, ALU.mult, ALU.add, ["u2"], ["u4"], K)
            tt(fl["dmu%d" % nx], u4, fl["dmu%d" % m], ALU.mult, ["u4", "dmu%d" % m], ["dmu%d" % nx], 64)
        p["tag"] = "up%d" % m
        first = min(m, 1)
        gat2(lambda a, b: T.w1[:, 513 + a:513 + b], T.ids[:, 0:961], zo, 0, ["idl", "idz", "idc", "zo%d" % m], "w1", CUTS["w"][first])
        gat2(into("p0"), T.w1[:, 0:961], zo, 0, ab("w1") + ["w1i", "zo%d" % m], "p0", CUTS["w"][first])
        a, b, c = 0, 1, 2
        for lv in range(LV):
            A_, B_, C_ = ["p%d" % i for i in (a, b, c)]
            o = K * lv
            s, sk = relay2(A_, "sc", CUTS["c" if lv else "w"][first] if SPLIT else 0)
            ts(T.offw[:, o:o + K], s, cp, -512.0, ALU.mult, ALU.add, sk + ["cp"], ["offw%d" % lv], K)
            gat2(into(B_), win(A_, 0, 450), T.offw, o, ab(A_) + [A_ + "i", A_ + "j", "offw%d" % lv], B_, CUTS["b"][first])
            gat2(into(C_), win(B_, 0, 450), T.offw, o, ab(B_) + [B_ + "i", B_ + "j", "offw%d" % lv], C_, CUTS["c"][first])
            a, c = c, a
        A_ = "p%d" % a
        if m == 0:
            ring_ops()
        gat2(lambda a, b: T.vr[:, a:b], win(A_, 0, 450), T.rw, 0, ab(A_) + [A_ + "i", A_ + "j"] + RW, "vr", CUTS["r"])
        v(lambda: V.tensor_tensor_scan(win("st", 1, 449), T.vr[:], T.mono[:], 512.0, ALU.max, ALU.min), ab("vr") + MONO, ["st"], L)
        gat2(into("bwin"), win("st", 0, 449), T.pmw, 0, ["st", "sti", "pmw"], "bwin", CUTS["r"])
        s, sk = relay2("bwin", "sc", CUTS["r"] if SPLIT else 0)
        places(T.sc, sk, T["bw%d" % m], "bw%d" % m, 0)
        send(dst, T["lbw%d" % m][:], T["bw%d" % m][:], "rb%d" % m, ["bw%d" % m], [], 0, "out_b%d" % m)
        arrive("rb%d" % m, n8, ["out_b%d" % m], ["lbw%d" % m], 2.0)
        p["tag"] = "e%d" % m
        gat2(lambda a, b: T.eb[:, a:b], win("bwin", 0, 449), T["liv%d" % m], 0, ab("bwin") + ["bwini", "liv%d" % m], "eb", 0)
        relay(T.eb[:], T.scb, "scb", ab("eb"))
        places(T.scb, ["scb"], T["ew%d" % m], "ew%d" % m, 1)
        send(dst, T["lew%d" % m][:], T["ew%d" % m][:], "re_%d" % m, ["ew%d" % m], [], 0, "out_e%d" % m)
        arrive("re_%d" % m, n8, ["out_e%d" % m], ["lew%d" % m], 2.0)
        p["tag"] = "to%d" % m
        for b in range(4):
            mm(b, T.eqc, T.eqp, 128 * b, xc, xp, 0, L, X + ["eq%d" % b])
            unload(b, T.to[:, TW * b + 1:TW * b + 449], L, 1.0, ["to%d" % b])
        p["tag"] = "tp%d" % m
        for b in range(4):
            mm(4 + b, T.eqc, T.eqp, 128 * b, lc, lp, 0, L, ["la%d" % m, "eq%d" % b])
            unload(4 + b, T.tp[:, TW * b + 1:TW * b + 449], L, 1.0, ["tp%d" % b])
        p["tag"] = "ga%d" % m
        for b in range(4):
            for c0, c1 in PARTS:
                gat(T.g1[:, L * b + c0:L * b + c1], T.tp[:, TW * b:TW * b + 449], T["liv%d" % m][:, c0 // 16:c1 // 16],
                    ["tp%d" % b, "tpi%d" % b, "liv%d" % m], ["g1%d_%d" % (b, c0)], c1 - c0, G1)
        p["tag"] = "gb%d" % m
        for b in range(4):
            for c0, c1 in PARTS:
                gat(T.g2[:, L * b + c0:L * b + c1], T.to[:, TW * b:TW * b + 449], T["udw%d" % m][:, c0 // 16:c1 // 16],
                    ["to%d" % b, "toi%d" % b, "udw%d" % m], ["g2%d_%d" % (b, c0)], c1 - c0)
        p["tag"] = ""
        for h, (c0, c1) in enumerate(((0, CUT), (CUT, L))):
            for b in range(4):
                v(lambda b=b, c0=c0, c1=c1, m=m: V.tensor_tensor(T.zt[:, 4 * c0 + b:4 * c1:4], T.tp[:, TW * b:TW * b + 449].indirect(T["lbw%d" % m][:, c0 // 16:c1 // 16]),
                                                                 T.g1[:, L * b + c0:L * b + c1], ALU.add),
                  ["tp%d" % b, "tpi%d" % b, "lbw%d" % m, "g1%d_%d" % (b, c0)], ["zt%d%d" % (h, b)], 60, c1 - c0)
            v(lambda c0=c0, c1=c1: V.quantize_mx(T.zqc[:, c0:c1], T.zqp[:, c0:c1], T.zt[:, 4 * c0:4 * c1]), ["zt%d%d" % (h, b) for b in range(4)], ["zq%d" % h], 14 + (c1 - c0) * 1.06)
            for b in range(4):
                i = 4 * h + b
                mm(i, T.wqc, T.wqp, 128 * b, T.zqc, T.zqp, c0, c1, ["wqc", "wqp", "zq%d" % h])
                unload(i, T.hh[:, TW * b + 1 + c0:TW * b + 1 + c1], c1 - c0, 0.015625, ["hh%d%d" % (b, h)])
        for b in range(4):
            v(lambda b=b, m=m: V.tensor_tensor(T.xnt[:, b:4 * L:4], T.hh[:, TW * b:TW * b + 449].indirect(T["lew%d" % m][:, 0:K]), T.g2[:, L * b:L * b + L], ALU.add),
              ["hh%d0" % b, "hh%d1" % b, "hhi%d" % b, "lew%d" % m] + ["g2%d_%d" % (b, c0) for c0, c1 in PARTS], ["xnt%d" % b], 60, L)
        v(lambda nx=nx: V.quantize_mx(T["xqc%d" % nx][:], T["xqp%d" % nx][:], T.xnt[:]), ["xnt%d" % b for b in range(4)], ["xq%da" % nx, "xq%db" % nx], 14 + L * 1.06)

    outs = [0]

    def store(q, out, in_, r):
        outs[0] += 16
        add(p, (q,), lambda e: (g.sync if e == "S" else g.scalar).dma_start(out, in_), r, ["st%d" % outs[0]], 0.05, 2.0, "d", "d_out")
    X = ["xq3a", "xq3b"]
    gat2(lambda a, b: T.uf0[:, a:b], T.ids[:, 512:961], T["udw%d" % (NR - 1)], 0, ["udw%d" % (NR - 1), "idc", "idz"], "uf0", 0)
    ts(T.uf[:], T.uf0[:], -513.0, None, ALU.add, None, ab("uf0"), ["uf"], L)
    store("S", T.uo[:], T.uf[0:128:16, :], ["uf"])
    v(lambda: V.quantize_mx(T.vqc[:], T.vqp[:], T.vt[:]), ["vt"], ["vq"], 140)
    mm(4, T.vqc, T.vqp, 0, T.xqc3, T.xqp3, 0, L, X + ["vq"])
    unload(4, T.ysb[:], L, 1.0, ["ysb"])
    store("S", T.oc[:], T.xqc3[:].bitcast(U8), X)
    for k in range(4):
        store("AS"[k % 2], T.osc[4 * k:4 * k + 4, 0:L], T.xqp3[32 * k:32 * k + 4, 0:L], X)
    store("A", T.y[:], T.ysb[:], ["ysb"])
    return p, sent, outs, n8


def rank_program(g, core, T, topo):
    rank = T.rank_of(core)
    if rank is None:
        return
    p, sent, outs, n8 = build(g, core, T, topo)
    count = emit(g, T, p)
    for e, s in SEM.items():
        if count[e]:
            g.wait_ge(T.sem[s], count[e])
    for s in LOADS:
        g.wait_ge(T.sem[s], 16)
    g.wait_ge(T.sem.d_out, outs[0])
    for m in range(NR):
        for a, k in (("rc", 2), ("ri", 1), ("rb", 1), ("re_", 1)):
            g.wait_ge(T.sem["%s%d" % (a, m)], k * n8)
    g.wait_ge(T.sem.sent, sent[0])
